import numpy as np
import ml_dtypes


def mxq(x, axis, fmt="e4m3"):
    dtype, down = {"e4m3": (ml_dtypes.float8_e4m3fn, 7), "e5m2": (ml_dtypes.float8_e5m2, 14)}[fmt]
    v = np.moveaxis(np.asarray(x, np.float32).astype(ml_dtypes.bfloat16).astype(np.float64), axis, -1)
    blocks = v.reshape(v.shape[:-1] + (-1, 32))
    amax = np.abs(blocks).max(-1, keepdims=True)
    byte = np.maximum(np.where(amax > 0, np.frexp(amax)[1] - 1 + 127, 0) - down, 1)
    scale = np.exp2(byte - 127.0)
    codes = (blocks / scale).astype(np.float32).astype(dtype).astype(np.float64)
    return np.moveaxis((codes * scale).reshape(v.shape), -1, axis)


WIDE = False


def mx_kscale(k):
    if not WIDE:
        return np.ones(k)
    levels = np.array([10, -10, 5, -5, 0])
    if k % 512:
        return np.exp2(np.random.permutation(np.resize(levels, k // 32))).repeat(32)
    a = np.empty((k // 512, 16))
    for p in range(k // 512):
        a[p, :8] = np.random.permutation(np.resize(levels, 8))
        for g in range(8):
            far = levels[np.abs(levels - a[p, g]) >= 10]
            a[p, g + 8] = far[np.random.randint(len(far))]
    return np.exp2(a.ravel()).repeat(32)


BF16 = ml_dtypes.bfloat16


def bf(x):
    return np.asarray(x, np.float32).astype(BF16)


def f64(x):
    return np.asarray(x).astype(np.float64)

def planes(Y):
    n, m = Y.shape
    b = f64(bf(Y)).reshape(n // 32, 32, m)
    amax = np.abs(b).max(1)
    byte = np.clip(np.where(amax > 0, np.frexp(amax)[1] - 1 + 127 - 7, 1), 1, 254)
    codes = (b * np.exp2(127.0 - byte)[:, None, :]).reshape(n, m).astype(np.float32).astype(ml_dtypes.float8_e4m3fn).view(np.uint8)
    words = codes.reshape(n // 512, 128, 4, m).transpose(0, 1, 3, 2)
    return np.ascontiguousarray(words), np.ascontiguousarray(byte.astype(np.uint8).reshape(n // 512, 16, m))


A, S, P, B = 512, 2048, 1024, 1536

def setup_inputs():
    r = np.random.randn
    s = mx_kscale(A)
    t = mx_kscale(S)
    amounts = np.exp(r(P, A)) * np.exp(0.5 * r(P, 1))
    coeffs = 0.3 / A * np.exp(r(S, A)) * np.exp(0.6 * r(S, 1))
    contrast = 2.0 / np.sqrt(S) * r(S, B)
    return {
        "profiles": bf(amounts * s),
        "absorption": bf(coeffs / s),
        "band_weights": bf(np.exp(0.3 * r(S)) * t),
        "contrast": bf(contrast / t[:, None]),
        "offset": bf(0.5 * r(B)),
        "gain": bf(np.exp(0.8 * r(B))),
        "angle_factor": bf(np.exp(0.2 * r(P))),
    }

def reference(profiles, absorption, band_weights, contrast, offset, gain, angle_factor):
    tau = mxq(f64(absorption), 1, "e4m3") @ mxq(f64(profiles), 1, "e4m3").T
    h = np.exp(-tau) * f64(band_weights)[:, None]
    flux = mxq(h, 0, "e4m3").T @ mxq(f64(contrast), 0, "e4m3")
    y = (flux + f64(offset)) * f64(gain) * f64(angle_factor)[:, None]
    Y = y.T
    words, scales = planes(Y)
    return y, words, scales

@@ -1,0 +1,421 @@
+from contextlib import ExitStack
+
+import concourse.mybir as mybir
+from concourse.masks import make_identity
+
+A, S, J, B = 512, 2048, 1024, 1536
+FLOPS = 2 * S * A * J + 2 * J * S * B
+
+F32 = mybir.dt.float32
+BF16 = mybir.dt.bfloat16
+U32 = mybir.dt.uint32
+I32 = mybir.dt.int32
+U8 = mybir.dt.uint8
+FP8X4 = mybir.dt.float8_e4m3fn_x4
+ACT = mybir.ActivationFunctionType
+ALU = mybir.AluOpType
+
+P = 128
+G = S // 512
+NQ = J // 256
+NC = B // 512
+
+MANUAL = False
+STEPS = "q0 c0 c1 q1 c2 c3 q2 c4 c5 q3"
+KINDS = "ccccccrcrcrr"
+CAST_S = "111100000011"
+RATE = 1
+HEAD = 0
+E_BUFS = 6
+PLANE_LAG = 4
+WHOLE_FROM = 1
+P_EARLY = 0
+SCALAR_PIECES = ((2, 0), (2, 1))
+SLACK = 0
+
+
+def tile_spectral_transmittance_channel_flux_h3_kernel(
+    tc, profiles, absorption, band_weights, contrast, offset, gain, angle_factor, out_0, out_1, out_2
+):
+    nc = tc.nc
+    with ExitStack() as ctx:
+        keep = ctx.enter_context(tc.tile_pool(name="keep", bufs=1))
+        work = ctx.enter_context(tc.tile_pool(name="work", bufs=3))
+        psum = ctx.enter_context(tc.psum_pool(name="psum", bufs=8))
+        if MANUAL:
+            ctx.enter_context(tc.manual_schedule())
+
+        steps = [(s[0], int(s[1])) for s in STEPS.split()]
+        halves = []
+        have = {"q": [], "c": []}
+        for kind, n in steps:
+            have[kind].append(n)
+            if kind == "q":
+                halves.extend((ch, n) for ch in have["c"])
+            else:
+                halves.extend((n, q) for q in have["q"])
+        units = [(ch // 2, q) for ch, q in halves if ch % 2 == 1]
+        row_units = [u for u, kind in zip(units, KINDS) if kind == "r"]
+        cast_scalar = [u for u, kind in zip(units, CAST_S) if kind == "1"]
+        row_groups = sorted({cg for cg, q in row_units})
+
+        def bank(shape, name):
+            return psum.tile(shape, F32, name=name, tag="bank")
+
+        raw = {}
+
+        def load_profiles(q):
+            raw["p", q] = keep.tile([P, 2, A], BF16, name="raw_p%d" % q)
+            nc.sync.dma_start(out=raw["p", q][:], in_=profiles[256 * q : 256 * q + 256, :].rearrange("(t m) k -> m t k", t=2))
+
+        def load_absorption(g):
+            raw["a", g] = keep.tile([P, 4, A], BF16, name="raw_a%d" % g, tag="big", bufs=16)
+            nc.sync.dma_start(out=raw["a", g][:], in_=absorption[512 * g : 512 * g + 512, :].rearrange("(m t) k -> m t k", t=4))
+
+        def load_contrast(g, cg):
+            raw["c", g, cg] = keep.tile([P, 4, 512], BF16, name="raw_c%d_%d" % (g, cg), tag="big", bufs=16)
+            nc.sync.dma_start(
+                out=raw["c", g, cg][:],
+                in_=contrast[512 * g : 512 * g + 512, 512 * cg : 512 * cg + 512].rearrange("(p t) c -> p t c", t=4),
+            )
+
+        ident = keep.tile([P, P], F32, name="ident")
+        make_identity(nc, ident[:])
+        rows32 = keep.tile([P, P], F32, name="rows32")
+        nc.gpsimd.memset(rows32[:], 0.0)
+        weights = keep.tile([P, G, 4], BF16, name="weights")
+        rows16 = keep.tile([32, P], BF16, name="rows16")
+        cols = keep.tile([P, 32], F32, name="cols")
+        shift = keep.tile([P, 12], F32, name="shift")
+        spread = {}
+
+        if HEAD == 1:
+            load_contrast(0, 0)
+        load_profiles(0)
+        if HEAD == 2:
+            load_contrast(0, 0)
+        load_absorption(0)
+        nc.sync.dma_start(out=weights[:], in_=band_weights.rearrange("(g p t) -> p g t", g=G, t=4))
+        for g in range(G):
+            if g > 0 or HEAD == 0:
+                load_contrast(g, 0)
+            if g + 1 < G:
+                load_absorption(g + 1)
+        nc.sync.dma_start(out=rows16[0:12, :], in_=gain.rearrange("(r i) -> r i", i=P))
+        nc.sync.dma_start(out=rows16[12:24, :], in_=offset.rearrange("(r i) -> r i", i=P))
+        nc.sync.dma_start(out=rows16[24:32, :], in_=angle_factor.rearrange("(r i) -> r i", i=P))
+        for kind, n in steps[2:]:
+            if kind == "q":
+                load_profiles(n)
+            elif n % 2 == 0:
+                for g in range(G):
+                    load_contrast(g, n // 2)
+        lo, hi = 512 * row_groups[0], 512 * row_groups[-1] + 512
+        for name, vec in (("gain", gain), ("offset", offset)):
+            spread[name] = keep.tile([P, hi - lo], BF16, name="spread_" + name)
+            nc.sync.dma_start(out=spread[name][:], in_=vec[lo:hi].partition_broadcast(P))
+
+        p_codes = keep.tile([P, J], U32, name="p_codes", align_bytes=64)
+        p_scales = keep.tile([P, J], U8, name="p_scales", align_bytes=64)
+        a_codes, a_scales, h_codes, h_scales, c_codes, c_scales = {}, {}, {}, {}, {}, {}
+        for g in range(G):
+            a_codes[g] = keep.tile([P, 512], U32, name="a_codes%d" % g, align_bytes=64)
+            a_scales[g] = keep.tile([P, 512], U8, name="a_scales%d" % g, align_bytes=64)
+            h_codes[g] = keep.tile([P, J], U32, name="h_codes%d" % g, align_bytes=64)
+            h_scales[g] = keep.tile([P, J], U8, name="h_scales%d" % g, align_bytes=64)
+            c_codes[g] = keep.tile([P, B], U32, name="c_codes%d" % g, align_bytes=64)
+            c_scales[g] = keep.tile([P, B], U8, name="c_scales%d" % g, align_bytes=64)
+        y_scales = keep.tile([P, J], U8, name="y_scales", align_bytes=64)
+
+        def quantize(codes, scales, grouped):
+            nc.vector.quantize_mx(out=codes.bitcast(FP8X4), scales=scales, in_=grouped)
+
+        def matmul(out, lhs, lhs_scale, rhs, rhs_scale, start, stop):
+            nc.tensor.matmul_mx(
+                out=out, lhsT=lhs.bitcast(FP8X4), lhsT_scale=lhs_scale, rhs=rhs.bitcast(FP8X4), rhs_scale=rhs_scale,
+                start=start, stop=stop,
+            )
+
+        live = {}
+
+        def turn_item(key, slots, codes, scales):
+            def turn():
+                for pair in range(slots // 2):
+                    live[key, pair] = bank([P, 2, 2, P], "turned")
+                    for t in range(2):
+                        words = raw[key][:, 2 * pair + t, :].bitcast(F32)
+                        for u in range(2):
+                            nc.tensor.transpose(live[key, pair][:, t, u, :], words[:, u:256:2], ident[:])
+
+            def leave():
+                live[key] = work.tile([P, slots * 512], BF16, name="grouped", tag="grouped", align_bytes=64)
+                for pair in range(slots // 2):
+                    words = live[key][:].bitcast(F32)[:, 512 * pair : 512 * pair + 512]
+                    nc.scalar.copy(
+                        out=words.rearrange("p (t m u) -> p t m u", t=2, u=2),
+                        in_=live[key, pair][:].rearrange("p t u m -> p t m u"),
+                    )
+
+            def pack():
+                quantize(codes, scales, live[key][:])
+
+            return [], [("tr", turn), ("", leave), ("", pack)], key
+
+        def constants_item():
+            def widen():
+                nc.vector.tensor_copy(out=rows32[0:32, :], in_=rows16[:])
+
+            def turn():
+                live["k"] = bank([P, P], "turned_rows")
+                nc.tensor.transpose(live["k"][:], rows32[:], ident[:])
+
+            def leave():
+                nc.scalar.copy(out=cols[:], in_=live["k"][:, 0:32])
+
+            def product():
+                nc.vector.tensor_tensor(out=shift[:], in0=cols[:, 0:12], in1=cols[:, 12:24], op=ALU.mult)
+
+            return [], [("", widen), ("tr", turn), ("", leave), ("", product)], "k"
+
+        def contrast_item(g, ch):
+            cg = ch // 2
+            whole = cg >= WHOLE_FROM
+            key = ("c", g, cg if whole else (ch, "half"))
+            width = 512 if whole else 256
+            first = 0 if whole else 256 * (ch % 2)
+
+            def weave():
+                live[key] = work.tile([P, 4 * width], BF16, name="grouped", tag="grouped", align_bytes=64)
+                copy = nc.scalar.copy if (g, ch) in SCALAR_PIECES else nc.vector.tensor_copy
+                copy(
+                    out=live[key][:].rearrange("p (c i t) -> p c t i", i=4, t=4),
+                    in_=raw["c", g, cg][:, :, first : first + width].rearrange("p t (c i) -> p c t i", i=4),
+                )
+
+            def pack():
+                window = slice(512 * cg + first, 512 * cg + first + width)
+                quantize(c_codes[g][:, window], c_scales[g][:, window], live[key][:])
+
+            return [], [("", weave), ("", pack)], key
+
+        def transmittance_item(g, q):
+            key = ("h", g, q)
+
+            def depth():
+                for jt in range(2):
+                    live[key, jt] = bank([P, 4, P], "tau")
+                    window = slice(256 * q + P * jt, 256 * q + P * jt + P)
+                    for t in range(4):
+                        slot = slice(P * t, P * t + P)
+                        matmul(live[key, jt][:, t, :], a_codes[g][:, slot], a_scales[g][:, slot],
+                               p_codes[:, window], p_scales[:, window], True, True)
+
+            def decay():
+                live[key, "e"] = work.tile([P, 256, 4], F32, name="decay", bufs=E_BUFS)
+                for jt in range(2):
+                    nc.scalar.activation(
+                        out=live[key, "e"][:, P * jt : P * jt + P, :], in_=live[key, jt][:].rearrange("p t n -> p n t"),
+                        func=ACT.Exp, scale=-1.0,
+                    )
+
+            def weigh():
+                live[key] = work.tile([P, 256, 4], BF16, name="weighed", align_bytes=64)
+                nc.vector.tensor_tensor(
+                    out=live[key][:], in0=live[key, "e"][:], in1=weights[:, g : g + 1, :].to_broadcast([P, 256, 4]),
+                    op=ALU.mult,
+                )
+
+            def pack():
+                window = slice(256 * q, 256 * q + 256)
+                quantize(h_codes[g][:, window], h_scales[g][:, window], live[key][:].rearrange("p n t -> p (n t)"))
+
+            return [("a", g), ("p", q)], [("mm", depth), ("", decay), ("", weigh), ("", pack)], key
+
+        def operands(cg, q, chs):
+            keys = [cg] if cg >= WHOLE_FROM else [(ch, "half") for ch in chs]
+            return [("h", g, q) for g in range(G)] + [("c", g, x) for g in range(G) for x in keys] + ["k"]
+
+        def column_item(cg, q, half):
+            key = ("z", cg, q, half)
+
+            def product():
+                live[key] = bank([P, 2, 256], "flux_t")
+                window = slice(256 * q, 256 * q + 256)
+                for i in range(2):
+                    ct = 4 * cg + 2 * half + i
+                    slot = slice(P * ct, P * ct + P)
+                    for g in range(G):
+                        matmul(live[key][:, i, :], c_codes[g][:, slot], c_scales[g][:, slot],
+                               h_codes[g][:, window], h_scales[g][:, window], g == 0, g == G - 1)
+
+            def leave():
+                if half == 0:
+                    live["z", cg, q] = work.tile([P, 4, 256], F32, name="scaled", bufs=4)
+                for i in range(2):
+                    ct = 4 * cg + 2 * half + i
+                    nc.scalar.activation(
+                        out=live["z", cg, q][:, 2 * half + i, :], in_=live[key][:, i, :], func=ACT.Identity,
+                        scale=cols[:, ct : ct + 1], bias=shift[:, ct : ct + 1],
+                    )
+
+            return operands(cg, q, [2 * cg + half]), [("mm", product), ("", leave)], key
+
+        def back_item(cg, q):
+            key = ("y", cg, q, 1)
+
+            def turn():
+                for jt in range(2):
+                    live[key, jt] = bank([P, 4, P], "turned_back")
+                    for i in range(4):
+                        nc.tensor.transpose(live[key, jt][:, i, :], live["z", cg, q][:, i, P * jt : P * jt + P], ident[:])
+
+            def leave():
+                live["y", cg, q] = keep.tile([P, 2, 512], F32, name="y", tag="big", bufs=16)
+                for jt in range(2):
+                    col = 24 + 2 * q + jt
+                    nc.scalar.activation(
+                        out=live["y", cg, q][:, jt, :], in_=live[key, jt][:].rearrange("p i c -> p (i c)"),
+                        func=ACT.Copy, scale=cols[:, col : col + 1],
+                    )
+
+            return [("z", cg, q, 0), ("z", cg, q, 1)], [("tr", turn), ("", leave)], key
+
+        def row_item(cg, q, jt):
+            key = ("y", cg, q, jt)
+            window = slice(512 * cg, 512 * cg + 512)
+            part = slice(512 * cg - lo, 512 * cg - lo + 512)
+
+            def product():
+                live[key] = bank([P, 512], "flux")
+                slot = slice(256 * q + P * jt, 256 * q + P * jt + P)
+                for g in range(G):
+                    matmul(live[key][:], h_codes[g][:, slot], h_scales[g][:, slot],
+                           c_codes[g][:, window], c_scales[g][:, window], g == 0, g == G - 1)
+
+            def shifted():
+                live[key, "t"] = work.tile([P, 512], F32, name="shifted")
+                nc.vector.tensor_tensor(out=live[key, "t"][:], in0=live[key][:], in1=spread["offset"][:, part], op=ALU.add)
+
+            def scaled():
+                if jt == 0:
+                    live["y", cg, q] = keep.tile([P, 2, 512], F32, name="y", tag="big", bufs=16)
+                col = 24 + 2 * q + jt
+                nc.vector.scalar_tensor_tensor(
+                    out=live["y", cg, q][:, jt, :], in0=live[key, "t"][:], scalar=cols[:, col : col + 1],
+                    in1=spread["gain"][:, part], op0=ALU.mult, op1=ALU.mult,
+                )
+
+            return operands(cg, q, [2 * cg, 2 * cg + 1]), [("mm", product), ("", shifted), ("", scaled)], key
+
+        def planes_item(cg, q):
+            key = ("w", cg, q)
+            window = slice(256 * q, 256 * q + 256)
+
+            def round_and_store():
+                y = live["y", cg, q]
+                nc.sync.dma_start(
+                    out=out_0[window, 512 * cg : 512 * cg + 512].rearrange("(t p) c -> p t c", t=2), in_=y[:]
+                )
+                live[key, "b"] = work.tile([P, 1024], BF16, name="rounded")
+                cast = nc.scalar.copy if (cg, q) in cast_scalar else nc.vector.tensor_copy
+                cast(
+                    out=live[key, "b"][:].rearrange("p (t u m e) -> p t u m e", t=2, u=2, e=2),
+                    in_=y[:].rearrange("p t (m u e) -> p t u m e", u=2, e=2),
+                )
+
+            def turn():
+                live[key] = bank([P, 2, 2, P], "turned_y")
+                words = live[key, "b"][:].bitcast(F32)
+                for t in range(2):
+                    for u in range(2):
+                        at = 256 * t + P * u
+                        nc.tensor.transpose(live[key][:, t, u, :], words[:, at : at + P], ident[:])
+
+            def leave():
+                live[key, "g"] = work.tile([P, 1024], BF16, name="grouped_y", align_bytes=64)
+                nc.scalar.copy(
+                    out=live[key, "g"][:].bitcast(F32).rearrange("p (t m u) -> p t m u", t=2, u=2),
+                    in_=live[key][:].rearrange("p t u m -> p t m u"),
+                )
+
+            def pack():
+                live[key, "c"] = work.tile([P, 256], U32, name="y_codes", align_bytes=64)
+                quantize(live[key, "c"][:], y_scales[4 * cg : P, window], live[key, "g"][:])
+
+            def store():
+                words = out_1[cg].rearrange("p m t -> p (m t)").bitcast(I32)
+                nc.sync.dma_start(out=words[:, window], in_=live[key, "c"][:].bitcast(I32))
+
+            return [("y", cg, q, 1)], [("", round_and_store), ("tr", turn), ("", leave), ("", pack), ("", store)], key
+
+        def p_item(q):
+            window = slice(256 * q, 256 * q + 256)
+            return turn_item(("p", q), 2, p_codes[:, window], p_scales[:, window])
+
+        def a_item(g):
+            return turn_item(("a", g), 4, a_codes[g][:], a_scales[g][:])
+
+        make = [p_item(0), a_item(0), contrast_item(0, 0)]
+        for g in range(G):
+            if g + 1 < G:
+                make.append(a_item(g + 1))
+            else:
+                make.append(constants_item())
+            make.append(transmittance_item(g, 0))
+            if g + 1 < G:
+                make.append(contrast_item(g + 1, 0))
+        later = steps[2:]
+        for i, (kind, n) in enumerate(later):
+            if kind == "q":
+                if i == 0:
+                    make.insert(len(make) - 2, p_item(n))
+                make.extend(transmittance_item(g, n) for g in range(G))
+            elif n // 2 < WHOLE_FROM or n % 2 == 0:
+                make.extend(contrast_item(g, n) for g in range(G))
+            if i + 1 < len(later) and later[i + 1][0] == "q":
+                make.insert(len(make) - 3 - P_EARLY, p_item(later[i + 1][1]))
+
+        use, back, planes = [], [], []
+        for ch, q in halves:
+            cg = ch // 2
+            if (cg, q) not in row_units:
+                use.append(column_item(cg, q, ch % 2))
+            elif ch % 2 == 1:
+                use.extend(row_item(cg, q, jt) for jt in range(2))
+        for cg, q in units:
+            if (cg, q) not in row_units:
+                back.append(back_item(cg, q))
+            planes.append(planes_item(cg, q))
+
+        queues = [planes, back, use, make]
+        heads = [0, 0, 0, 0]
+        turns = [0, 1, 2] + [3] * RATE
+        ready = {}
+        running = []
+        tick = 0
+        while running or any(heads[i] < len(queues[i]) for i in range(4)):
+            for i in turns:
+                queue = queues[i]
+                if heads[i] < len(queue):
+                    needs, stages, key = queue[heads[i]]
+                    if all(ready.get(k, tick + 1) <= tick - (PLANE_LAG if i == 0 else 0) for k in needs):
+                        running.append((tick, stages, key))
+                        heads[i] = heads[i] + 1
+            calls = [stages[tick - start] for start, stages, key in running]
+            first, second = ("mm", "tr") if tick % 2 == 0 else ("tr", "mm")
+            for kind in ("", first, second):
+                for tag, call in calls:
+                    if tag == kind:
+                        call()
+            for start, stages, key in running:
+                if tick - start == len(stages) - 1:
+                    ready[key] = tick + 1
+            running = [item for item in running if tick - item[0] < len(item[1]) - 1]
+            tick = tick + 1
+
+        scale_rows = out_2.bitcast(I32)
+        for quadrant in range(4):
+            nc.sync.dma_start(
+                out=scale_rows[:, 4 * quadrant : 4 * quadrant + 4, :],
+                in_=y_scales[32 * quadrant : 32 * quadrant + 4 * NC, :].bitcast(I32),
+            )

@@ -20,17 +20,41 @@ G = S // 512
 NQ = J // 256
 NC = B // 512
 
-MANUAL = False
+MANUAL = True
 STEPS = "q0 c0 c1 q1 c2 c3 q2 c4 c5 q3"
-KINDS = "ccccccrcrcrr"
-CAST_S = "111100000011"
+KINDS = "cccccrrrrrrr"
+CAST_S = "1111111111100"
 RATE = 1
 HEAD = 0
 E_BUFS = 6
-PLANE_LAG = 4
-WHOLE_FROM = 1
+PLANE_LAG = 0
+WHOLE_FROM = 0
 P_EARLY = 0
-SCALAR_PIECES = ((2, 0), (2, 1))
+W_LAG = 3
+S_LAG = 2
+D_PER_ROUND = (4, 4, 2, 2)
+P_ROUND = (-1, 0)
+EARLY_TURN = (1,)
+SCALAR_AT = ()
+FRONT_ORDER = (("j", 0), ("qp", 0), ("w", 0, 0), ("qa", 0), ("qc", 0, 0), ("w", 1, 0), ("qa", 1), ("qc", 1, 0), ("w", 2, 0), ("qa", 2), ("qc", 2, 0))
+QP_AFTER = (("m", 0, 1), ("m", 0, 2))
+TW_ROUND = (6, 6, 7, 7, 8, 8, 9, 9, 10, 11, 12, 12, 13)
+Q_LAG = 1
+BANKS = 7
+G_WIDTH = 336
+UNITS = ((0, 0), (0, 1), (1, 0), (1, 1), (0, 2), (1, 2), (0, 3), (1, 3), (2, 0), (2, 1), (2, 2), (2, 3))
+SHADOWED = ((3, 0), (0, 1), (1, 1), (2, 1), (0, 2), (1, 2), (2, 2), (3, 2))
+GATES = ((2, 0), (3, 1))
+AFTER_PAIR = {0: [("qa", 3), ("k", 0), ("qp", 1)], 1: [("k", 3), ("qp", 2)], 3: [("qp", 3)]}
+GATE_AFTER = {3: [("w", 3, 1), ("qc", 3, 1)]}
+LATE_RY = 1
+C_LEAD = 0
+TENSOR_FRONT = (("tp", 0), ("ta", 0), ("j", 1), ("ta", 1), ("j", 3), ("d", 0, 0), ("ta", 2), ("d", 1, 0), ("ta", 3), ("tp", 1), ("d", 2, 0), ("tp", 2), ("d", 3, 0), ("k", 1))
+CS_BACK = 2
+INSERT = ()
+R_BUFS = 4
+Y_BUFS = 3
+SCALAR_PIECES = ()
 SLACK = 0
 
 
@@ -41,22 +65,13 @@ def tile_spectral_transmittance_channel_flux_h3_kernel(
     with ExitStack() as ctx:
         keep = ctx.enter_context(tc.tile_pool(name="keep", bufs=1))
         work = ctx.enter_context(tc.tile_pool(name="work", bufs=3))
-        psum = ctx.enter_context(tc.psum_pool(name="psum", bufs=8))
+        psum = ctx.enter_context(tc.psum_pool(name="psum", bufs=BANKS))
         if MANUAL:
             ctx.enter_context(tc.manual_schedule())
 
-        steps = [(s[0], int(s[1])) for s in STEPS.split()]
-        halves = []
-        have = {"q": [], "c": []}
-        for kind, n in steps:
-            have[kind].append(n)
-            if kind == "q":
-                halves.extend((ch, n) for ch in have["c"])
-            else:
-                halves.extend((n, q) for q in have["q"])
-        units = [(ch // 2, q) for ch, q in halves if ch % 2 == 1]
+        units = list(UNITS)
+        shadowed = list(SHADOWED)
         row_units = [u for u, kind in zip(units, KINDS) if kind == "r"]
-        cast_scalar = [u for u, kind in zip(units, CAST_S) if kind == "1"]
         row_groups = sorted({cg for cg, q in row_units})
 
         def bank(shape, name):
@@ -88,6 +103,10 @@ def tile_spectral_transmittance_channel_flux_h3_kernel(
         cols = keep.tile([P, 32], F32, name="cols")
         shift = keep.tile([P, 12], F32, name="shift")
         spread = {}
+        wide = keep.tile([P, P], F32, name="wide")
+        wide_t = keep.tile([P, P], F32, name="wide_t")
+        nc.gpsimd.memset(wide[:], 0.0)
+        held_weights = psum.tile([P, P], F32, name="held_weights", bufs=1)
 
         if HEAD == 1:
             load_contrast(0, 0)
@@ -104,12 +123,14 @@ def tile_spectral_transmittance_channel_flux_h3_kernel(
         nc.sync.dma_start(out=rows16[0:12, :], in_=gain.rearrange("(r i) -> r i", i=P))
         nc.sync.dma_start(out=rows16[12:24, :], in_=offset.rearrange("(r i) -> r i", i=P))
         nc.sync.dma_start(out=rows16[24:32, :], in_=angle_factor.rearrange("(r i) -> r i", i=P))
-        for kind, n in steps[2:]:
-            if kind == "q":
-                load_profiles(n)
-            elif n % 2 == 0:
-                for g in range(G):
-                    load_contrast(g, n // 2)
+        load_profiles(1)
+        load_contrast(0, 1)
+        load_profiles(2)
+        for g in range(1, G):
+            load_contrast(g, 1)
+        load_profiles(3)
+        for g in range(G):
+            load_contrast(g, 2)
         lo, hi = 512 * row_groups[0], 512 * row_groups[-1] + 512
         for name, vec in (("gain", gain), ("offset", offset)):
             spread[name] = keep.tile([P, hi - lo], BF16, name="spread_" + name)
@@ -159,7 +180,7 @@ def tile_spectral_transmittance_channel_flux_h3_kernel(
             def pack():
                 quantize(codes, scales, live[key][:])
 
-            return [], [("tr", turn), ("", leave), ("", pack)], key
+            return [], [("tr", turn), ("str", leave), ("v", pack)], key
 
         def constants_item():
             def widen():
@@ -175,28 +196,59 @@ def tile_spectral_transmittance_channel_flux_h3_kernel(
             def product():
                 nc.vector.tensor_tensor(out=shift[:], in0=cols[:, 0:12], in1=cols[:, 12:24], op=ALU.mult)
 
-            return [], [("", widen), ("tr", turn), ("", leave), ("", product)], "k"
+            return [], [("v", widen), ("tr", turn), ("str", leave), ("v", product)], "k"
 
-        def contrast_item(g, ch):
-            cg = ch // 2
-            whole = cg >= WHOLE_FROM
-            key = ("c", g, cg if whole else (ch, "half"))
-            width = 512 if whole else 256
-            first = 0 if whole else 256 * (ch % 2)
+        def weights_item():
+            def widen():
+                nc.vector.tensor_copy(out=wide[:, 0:16], in_=weights[:].rearrange("p g t -> p (g t)"))
+
+            def turn():
+                live["w1"] = bank([P, P], "turned_weights")
+                nc.tensor.transpose(live["w1"][:], wide[:], ident[:])
+
+            def leave():
+                nc.scalar.copy(out=wide_t[:], in_=live["w1"][:])
+
+            def back():
+                nc.tensor.transpose(held_weights[:], wide_t[:], ident[:])
+
+            return [], [("", widen), ("", turn), ("", leave), ("", back)], "w"
+
+        def contrast_item(g, cg):
+            key = ("c", g, cg)
+            shared = (g, cg) in shadowed
+            split = G_WIDTH if shared else 0
+
+            def tile():
+                if shared or (g, cg) in GATES:
+                    live[key] = work.tile([P, 2048], BF16, name="woven", bufs=1, align_bytes=64)
+                else:
+                    live[key] = work.tile([P, 2048], BF16, name="grouped", tag="grouped", align_bytes=64)
+
+            def weave_first():
+                tile()
+                if split:
+                    nc.gpsimd.tensor_scalar(
+                        out=live[key][:, : 4 * split].rearrange("p (c t) -> p c t", t=4),
+                        in0=raw[key][:, :, :split].rearrange("p t c -> p c t"),
+                        scalar1=1.0, scalar2=0.0, op0=ALU.mult, op1=ALU.add,
+                    )
 
             def weave():
-                live[key] = work.tile([P, 4 * width], BF16, name="grouped", tag="grouped", align_bytes=64)
-                copy = nc.scalar.copy if (g, ch) in SCALAR_PIECES else nc.vector.tensor_copy
-                copy(
-                    out=live[key][:].rearrange("p (c i t) -> p c t i", i=4, t=4),
-                    in_=raw["c", g, cg][:, :, first : first + width].rearrange("p t (c i) -> p c t i", i=4),
-                )
+                if not shared:
+                    tile()
+                copy = nc.scalar.copy if (g, cg) in SCALAR_PIECES else nc.vector.tensor_copy
+                if split < 512:
+                    copy(
+                        out=live[key][:, 4 * split :].rearrange("p (c i t) -> p c t i", i=4, t=4),
+                        in_=raw[key][:, :, split:].rearrange("p t (c i) -> p c t i", i=4),
+                    )
 
             def pack():
-                window = slice(512 * cg + first, 512 * cg + first + width)
+                window = slice(512 * cg, 512 * cg + 512)
                 quantize(c_codes[g][:, window], c_scales[g][:, window], live[key][:])
 
-            return [], [("", weave), ("", pack)], key
+            return weave_first, weave, pack
 
         def transmittance_item(g, q):
             key = ("h", g, q)
@@ -221,7 +273,7 @@ def tile_spectral_transmittance_channel_flux_h3_kernel(
             def weigh():
                 live[key] = work.tile([P, 256, 4], BF16, name="weighed", align_bytes=64)
                 nc.vector.tensor_tensor(
-                    out=live[key][:], in0=live[key, "e"][:], in1=weights[:, g : g + 1, :].to_broadcast([P, 256, 4]),
+                    out=live[key][:], in0=live[key, "e"][:], in1=held_weights[:, 4 * g : 4 * g + 4].unsqueeze(1).to_broadcast([P, 256, 4]),
                     op=ALU.mult,
                 )
 
@@ -229,11 +281,11 @@ def tile_spectral_transmittance_channel_flux_h3_kernel(
                 window = slice(256 * q, 256 * q + 256)
                 quantize(h_codes[g][:, window], h_scales[g][:, window], live[key][:].rearrange("p n t -> p (n t)"))
 
-            return [("a", g), ("p", q)], [("mm", depth), ("", decay), ("", weigh), ("", pack)], key
+            first = [("a", g), ("p", q)], [("mm", depth), ("smm", decay)], ("e", g, q)
+            return first, ([("e", g, q)], [("v", weigh), ("v", pack)], key)
 
         def operands(cg, q, chs):
-            keys = [cg] if cg >= WHOLE_FROM else [(ch, "half") for ch in chs]
-            return [("h", g, q) for g in range(G)] + [("c", g, x) for g in range(G) for x in keys] + ["k"]
+            return []
 
         def column_item(cg, q, half):
             key = ("z", cg, q, half)
@@ -258,7 +310,7 @@ def tile_spectral_transmittance_channel_flux_h3_kernel(
                         scale=cols[:, ct : ct + 1], bias=shift[:, ct : ct + 1],
                     )
 
-            return operands(cg, q, [2 * cg + half]), [("mm", product), ("", leave)], key
+            return operands(cg, q, [2 * cg + half]), [("mm", product), ("smm", leave)], key
 
         def back_item(cg, q):
             key = ("y", cg, q, 1)
@@ -278,7 +330,7 @@ def tile_spectral_transmittance_channel_flux_h3_kernel(
                         func=ACT.Copy, scale=cols[:, col : col + 1],
                     )
 
-            return [("z", cg, q, 0), ("z", cg, q, 1)], [("tr", turn), ("", leave)], key
+            return [("z", cg, q, 0), ("z", cg, q, 1)], [("tr", turn), ("str", leave)], key
 
         def row_item(cg, q, jt):
             key = ("y", cg, q, jt)
@@ -305,117 +357,211 @@ def tile_spectral_transmittance_channel_flux_h3_kernel(
                     in1=spread["gain"][:, part], op0=ALU.mult, op1=ALU.mult,
                 )
 
-            return operands(cg, q, [2 * cg, 2 * cg + 1]), [("mm", product), ("", shifted), ("", scaled)], key
+            return operands(cg, q, [2 * cg, 2 * cg + 1]), [("mm", product), ("v", shifted), ("v", scaled)], key
 
-        def planes_item(cg, q):
-            key = ("w", cg, q)
-            window = slice(256 * q, 256 * q + 256)
+        def planes_item(cg, q, first, count, by_scalar):
+            key = ("w", cg, q, first)
+            window = slice(256 * q + P * first, 256 * q + P * (first + count))
+            tiles = slice(first, first + count)
 
-            def round_and_store():
-                y = live["y", cg, q]
+            def store_y():
                 nc.sync.dma_start(
-                    out=out_0[window, 512 * cg : 512 * cg + 512].rearrange("(t p) c -> p t c", t=2), in_=y[:]
+                    out=out_0[window, 512 * cg : 512 * cg + 512].rearrange("(t p) c -> p t c", t=count),
+                    in_=live["y", cg, q][:, tiles, :],
                 )
-                live[key, "b"] = work.tile([P, 1024], BF16, name="rounded")
-                cast = nc.scalar.copy if (cg, q) in cast_scalar else nc.vector.tensor_copy
+
+            def round_y():
+                live[key, "b"] = work.tile([P, 512 * count], BF16, name="rounded", bufs=R_BUFS)
+                cast = nc.scalar.copy if by_scalar else nc.vector.tensor_copy
                 cast(
-                    out=live[key, "b"][:].rearrange("p (t u m e) -> p t u m e", t=2, u=2, e=2),
-                    in_=y[:].rearrange("p t (m u e) -> p t u m e", u=2, e=2),
+                    out=live[key, "b"][:].rearrange("p (t u m e) -> p t u m e", t=count, u=2, e=2),
+                    in_=live["y", cg, q][:, tiles, :].rearrange("p t (m u e) -> p t u m e", u=2, e=2),
                 )
 
             def turn():
-                live[key] = bank([P, 2, 2, P], "turned_y")
+                live[key] = bank([P, count, 2, P], "turned_y")
                 words = live[key, "b"][:].bitcast(F32)
-                for t in range(2):
+                for t in range(count):
                     for u in range(2):
                         at = 256 * t + P * u
                         nc.tensor.transpose(live[key][:, t, u, :], words[:, at : at + P], ident[:])
 
             def leave():
-                live[key, "g"] = work.tile([P, 1024], BF16, name="grouped_y", align_bytes=64)
+                live[key, "g"] = work.tile([P, 512 * count], BF16, name="grouped_y", bufs=R_BUFS, align_bytes=64)
                 nc.scalar.copy(
-                    out=live[key, "g"][:].bitcast(F32).rearrange("p (t m u) -> p t m u", t=2, u=2),
+                    out=live[key, "g"][:].bitcast(F32).rearrange("p (t m u) -> p t m u", t=count, u=2),
                     in_=live[key][:].rearrange("p t u m -> p t m u"),
                 )
 
             def pack():
-                live[key, "c"] = work.tile([P, 256], U32, name="y_codes", align_bytes=64)
+                live[key, "c"] = work.tile([P, P * count], U32, name="y_codes", bufs=R_BUFS, align_bytes=64)
                 quantize(live[key, "c"][:], y_scales[4 * cg : P, window], live[key, "g"][:])
 
             def store():
                 words = out_1[cg].rearrange("p m t -> p (m t)").bitcast(I32)
                 nc.sync.dma_start(out=words[:, window], in_=live[key, "c"][:].bitcast(I32))
 
-            return [("y", cg, q, 1)], [("", round_and_store), ("tr", turn), ("", leave), ("", pack), ("", store)], key
+            return [round_y, turn, leave, pack, store, store_y]
 
-        def p_item(q):
+        ops = {}
+
+        def chain(names, item, extra):
+            needs, stages, key = item
+            before = list(extra)
+            for name, (tag, call) in zip(names, stages):
+                ops[name] = (before, call)
+                before = [name]
+
+        def held(cg, q, chs):
+            return [("qh", g, q) for g in range(G)] + [("qc", g, cg) for g in range(G)] + [("k", 3)]
+
+        for q in range(NQ):
             window = slice(256 * q, 256 * q + 256)
-            return turn_item(("p", q), 2, p_codes[:, window], p_scales[:, window])
-
-        def a_item(g):
-            return turn_item(("a", g), 4, a_codes[g][:], a_scales[g][:])
-
-        make = [p_item(0), a_item(0), contrast_item(0, 0)]
+            chain([(n, q) for n in ("tp", "xp", "qp")], turn_item(("p", q), 2, p_codes[:, window], p_scales[:, window]), [])
         for g in range(G):
-            if g + 1 < G:
-                make.append(a_item(g + 1))
+            chain([(n, g) for n in ("ta", "xa", "qa")], turn_item(("a", g), 4, a_codes[g][:], a_scales[g][:]), [])
+            for cg in range(NC):
+                first, weave, pack = contrast_item(g, cg)
+                if (g, cg) in shadowed:
+                    ops["g", g, cg] = ([], first)
+                ops["w", g, cg] = ([("g", g, cg)] if (g, cg) in shadowed else [], weave)
+                ops["qc", g, cg] = ([("w", g, cg)], pack)
+            for q in range(NQ):
+                first, second = transmittance_item(g, q)
+                chain([("d", g, q), ("e", g, q)], first, [("qa", g), ("qp", q)])
+                chain([("m", g, q), ("qh", g, q)], second, [("e", g, q)])
+        chain([("k", i) for i in range(4)], constants_item(), [])
+        chain([("j", i) for i in range(4)], weights_item(), [])
+        for g in range(G):
+            for q in range(NQ):
+                ops["m", g, q][0].append(("j", 3))
+        for u, (cg, q) in enumerate(units):
+            if (cg, q) in row_units:
+                for jt in range(2):
+                    chain([("z", u, jt), ("rs", u, jt), ("ry", u, jt)], row_item(cg, q, jt), held(cg, q, [2 * cg, 2 * cg + 1]))
+                done = [("ry", u, 0), ("ry", u, 1)]
             else:
-                make.append(constants_item())
-            make.append(transmittance_item(g, 0))
-            if g + 1 < G:
-                make.append(contrast_item(g + 1, 0))
-        later = steps[2:]
-        for i, (kind, n) in enumerate(later):
-            if kind == "q":
-                if i == 0:
-                    make.insert(len(make) - 2, p_item(n))
-                make.extend(transmittance_item(g, n) for g in range(G))
-            elif n // 2 < WHOLE_FROM or n % 2 == 0:
-                make.extend(contrast_item(g, n) for g in range(G))
-            if i + 1 < len(later) and later[i + 1][0] == "q":
-                make.insert(len(make) - 3 - P_EARLY, p_item(later[i + 1][1]))
+                for half in range(2):
+                    chain([("z", u, half), ("zx", u, half)], column_item(cg, q, half), held(cg, q, [2 * cg + half]))
+                chain([("b", u), ("bx", u)], back_item(cg, q), [("zx", u, 0), ("zx", u, 1)])
+                done = [("bx", u)]
+            pieces = [(u, 0, 2, done)] if u + 1 < len(units) else [(u, 0, 1, done[:1]), (u + 1, 1, 1, done[1:])]
+            for part, first, count, needs in pieces:
+                stages = planes_item(cg, q, first, count, CAST_S[part] == "1")
+                chain([(n, part) for n in ("c", "tw", "xw", "qy", "sw")], ([], [("", s) for s in stages[:5]], 0), needs)
+                ops["sy", part] = (needs, stages[5])
 
-        use, back, planes = [], [], []
-        for ch, q in halves:
-            cg = ch // 2
-            if (cg, q) not in row_units:
-                use.append(column_item(cg, q, ch % 2))
-            elif ch % 2 == 1:
-                use.extend(row_item(cg, q, jt) for jt in range(2))
-        for cg, q in units:
-            if (cg, q) not in row_units:
-                back.append(back_item(cg, q))
-            planes.append(planes_item(cg, q))
+        rows = [u for u in range(len(units)) if units[u] in row_units]
+        parts = len(units) + 1
+        by_scalar = [u for u in range(parts) if CAST_S[u] == "1"]
 
-        queues = [planes, back, use, make]
-        heads = [0, 0, 0, 0]
-        turns = [0, 1, 2] + [3] * RATE
-        ready = {}
-        running = []
-        tick = 0
-        while running or any(heads[i] < len(queues[i]) for i in range(4)):
-            for i in turns:
-                queue = queues[i]
-                if heads[i] < len(queue):
-                    needs, stages, key = queue[heads[i]]
-                    if all(ready.get(k, tick + 1) <= tick - (PLANE_LAG if i == 0 else 0) for k in needs):
-                        running.append((tick, stages, key))
-                        heads[i] = heads[i] + 1
-            calls = [stages[tick - start] for start, stages, key in running]
-            first, second = ("mm", "tr") if tick % 2 == 0 else ("tr", "mm")
-            for kind in ("", first, second):
-                for tag, call in calls:
-                    if tag == kind:
-                        call()
-            for start, stages, key in running:
-                if tick - start == len(stages) - 1:
-                    ready[key] = tick + 1
-            running = [item for item in running if tick - item[0] < len(item[1]) - 1]
-            tick = tick + 1
+        tensor = list(TENSOR_FRONT)
+        depths = [("d", g, q) for q in range(1, NQ) for g in range(G)]
+        at = 0
+        rounds = max(TW_ROUND) + 1
+        ends = []
+        for r in range(rounds):
+            count = D_PER_ROUND[r] if r < len(D_PER_ROUND) else 0
+            turns = []
+            if 1 <= r <= len(units) and r - 1 not in rows:
+                turns.append(("b", r - 1))
+            turns.extend(("tw", u) for u in range(parts) if TW_ROUND[u] == r)
+            for q in range(2, NQ):
+                if r == P_ROUND[q - 2]:
+                    turns.append(("tp", q))
+            mms = depths[at : at + count]
+            at = at + count
+            product = [("z", r, 0), ("z", r, 1)] if r < len(units) else []
+            if r in EARLY_TURN:
+                tensor.extend(mms + turns + product)
+            else:
+                tensor.extend(mms + product + turns)
+            ends.append(tensor[-1])
+
+        exits = {"tp": "xp", "ta": "xa", "d": "e", "z": "zx", "b": "bx", "tw": "xw"}
+        scalar = []
+        for name in tensor:
+            if name[0] in "kj":
+                if name[1] == 1:
+                    scalar.append((name[0], 2))
+            elif name[0] != "z" or name[1] not in rows:
+                scalar.append((exits[name[0]],) + name[1:])
+            for g, ch, after in SCALAR_AT:
+                if name == after:
+                    scalar.append(("w", g, ch))
+            if name in ends:
+                scalar.extend(("c", u) for u in by_scalar if TW_ROUND[u] == ends.index(name) + CS_BACK)
+
+        vector = list(FRONT_ORDER)
+        pairs = [(g, q) for q in range(NQ) for g in range(0, G, 2)]
+        for i, (g, q) in enumerate(pairs):
+            vector.extend([("m", g, q), ("m", g + 1, q)])
+            piece = shadowed[i]
+            ops[("g",) + piece][0].append(vector[-3])
+            extra = AFTER_PAIR.get(i, [])
+            vector.extend([("w",) + piece] + extra[:1] + [("qh", g, q), ("qh", g + 1, q)] + extra[1:])
+            vector.append(("qc",) + piece)
+            vector.extend(GATE_AFTER.get(i, []))
+        gpsimd = [("g",) + piece for piece in shadowed]
+        last = len(units) - 1
+        for r in range(rounds + 1):
+            casts = [("c", u) for u in range(parts) if TW_ROUND[u] == r + 1 and u not in by_scalar]
+            packs = [("qy", u) for u in range(parts) if TW_ROUND[u] == r - Q_LAG]
+            if r == rounds:
+                packs = [("qy", u) for u in range(parts) if TW_ROUND[u] >= r - Q_LAG]
+            line = [("ry", r - 1, 1)] if r - 1 in rows and LATE_RY and r - 1 < last else []
+            early = [c for c in casts if c[1] < r - 1 or not line]
+            late = [c for c in casts if c not in early]
+            if r == last:
+                line = line + packs + [("rs", r, 0), ("rs", r, 1), ("ry", r, 0)] + [c for c in casts if c[1] < r] + [("ry", r, 1)] + [c for c in casts if c[1] >= r]
+            elif r in rows and LATE_RY:
+                line = line + early[:1] + [("rs", r, 0)] + packs[:1] + [("rs", r, 1)] + packs[1:] + [("ry", r, 0)] + early[1:] + late
+            elif r in rows:
+                line = early[:1] + [("rs", r, 0)] + packs[:1] + [("rs", r, 1), ("ry", r, 0)] + packs[1:] + [("ry", r, 1)] + early[1:]
+            else:
+                line = line + casts + packs
+            vector.extend(name for name in line if name not in vector)
+
+        stores = []
+        for r in range(rounds + 1):
+            stores.extend(("sw", u) for u in range(parts) if TW_ROUND[u] == r - 1 - Q_LAG)
+            if 1 <= r <= parts:
+                stores.append(("sy", r - 1))
+        stores.extend(("sw", u) for u in range(parts) if ("sw", u) not in stores)
+
+        banks = []
+        for name in tensor:
+            if name[0] == "z" and name[1] in rows:
+                free = ("rs",) + name[1:]
+            elif name == ("j", 3):
+                continue
+            elif name[0] in "kj":
+                free = (name[0], 2)
+            else:
+                free = (exits[name[0]],) + name[1:]
+            count = 2 if name[0] in ("ta", "d", "b") else 1
+            ops[name][0].extend(banks[i] for i in range(len(banks) - BANKS, len(banks) - BANKS + count) if i >= 0)
+            banks.extend([free] * count)
+        decays = [name for name in scalar if name[0] == "e"]
+        for i in range(E_BUFS, len(decays)):
+            ops[decays[i]][0].append(("m",) + decays[i - E_BUFS][1:])
+
+        programs = [gpsimd, vector, scalar, tensor, stores]
+        heads = [0] * len(programs)
+        written = set()
+        while any(heads[i] < len(program) for i, program in enumerate(programs)):
+            moved = False
+            for i, program in enumerate(programs):
+                while heads[i] < len(program) and all(n in written for n in ops[program[heads[i]]][0]):
+                    ops[program[heads[i]]][1]()
+                    written.add(program[heads[i]])
+                    heads[i] = heads[i] + 1
+                    moved = True
+            assert moved, [program[heads[i] : heads[i] + 1] for i, program in enumerate(programs)]
 
         scale_rows = out_2.bitcast(I32)
         for quadrant in range(4):
-            nc.sync.dma_start(
+            nc.scalar.dma_start(
                 out=scale_rows[:, 4 * quadrant : 4 * quadrant + 4, :],
                 in_=y_scales[32 * quadrant : 32 * quadrant + 4 * NC, :].bitcast(I32),
             )

@@ -3,8 +3,8 @@ from contextlib import ExitStack
 import concourse.mybir as mybir
 from concourse.masks import make_identity
 
-A, S, J, B = 512, 2048, 1024, 1536
-FLOPS = 2 * S * A * J + 2 * J * S * B
+LAYERS, POINTS, PROFILES, CHANNELS = 512, 2048, 1024, 1536
+FLOPS = 2 * POINTS * LAYERS * PROFILES + 2 * PROFILES * POINTS * CHANNELS
 
 F32 = mybir.dt.float32
 BF16 = mybir.dt.bfloat16
@@ -16,46 +16,22 @@ ACT = mybir.ActivationFunctionType
 ALU = mybir.AluOpType
 
 P = 128
-G = S // 512
-NQ = J // 256
-NC = B // 512
+PASS = 512
+QUARTER = 256
+GROUPS = POINTS // PASS
+QUARTERS = PROFILES // QUARTER
+THIRDS = CHANNELS // PASS
+PATCHES = THIRDS * QUARTERS
+CHANNEL_TILES = CHANNELS // P
+PROFILE_TILES = PROFILES // P
 
-MANUAL = True
-STEPS = "q0 c0 c1 q1 c2 c3 q2 c4 c5 q3"
-KINDS = "cccccrrrrrrr"
-CAST_S = "1111111111100"
-RATE = 1
-HEAD = 0
-E_BUFS = 6
-PLANE_LAG = 0
-WHOLE_FROM = 0
-P_EARLY = 0
-W_LAG = 3
-S_LAG = 2
-D_PER_ROUND = (4, 4, 2, 2)
-P_ROUND = (-1, 0)
-EARLY_TURN = (1,)
-SCALAR_AT = ()
-FRONT_ORDER = (("j", 0), ("qp", 0), ("w", 0, 0), ("qa", 0), ("qc", 0, 0), ("w", 1, 0), ("qa", 1), ("qc", 1, 0), ("w", 2, 0), ("qa", 2), ("qc", 2, 0))
-QP_AFTER = (("m", 0, 1), ("m", 0, 2))
-TW_ROUND = (6, 6, 7, 7, 8, 8, 9, 9, 10, 11, 12, 12, 13)
-Q_LAG = 1
-BANKS = 7
-G_WIDTH = 336
-UNITS = ((0, 0), (0, 1), (1, 0), (1, 1), (0, 2), (1, 2), (0, 3), (1, 3), (2, 0), (2, 1), (2, 2), (2, 3))
-SHADOWED = ((3, 0), (0, 1), (1, 1), (2, 1), (0, 2), (1, 2), (2, 2), (3, 2))
-GATES = ((2, 0), (3, 1))
-AFTER_PAIR = {0: [("qa", 3), ("k", 0), ("qp", 1)], 1: [("k", 3), ("qp", 2)], 3: [("qp", 3)]}
-GATE_AFTER = {3: [("w", 3, 1), ("qc", 3, 1)]}
-LATE_RY = 1
-C_LEAD = 0
-TENSOR_FRONT = (("tp", 0), ("ta", 0), ("j", 1), ("ta", 1), ("j", 3), ("d", 0, 0), ("ta", 2), ("d", 1, 0), ("ta", 3), ("tp", 1), ("d", 2, 0), ("tp", 2), ("d", 3, 0), ("k", 1))
-CS_BACK = 2
-INSERT = ()
-R_BUFS = 4
-Y_BUFS = 3
-SCALAR_PIECES = ()
-SLACK = 0
+GPSIMD_CHANNELS = 344
+TURNED_PATCHES = 5
+FIRST_PLANES_ROUND = 6
+ROTATING_BANKS = 7
+LOAD_SLOTS = GROUPS + GROUPS * THIRDS
+TURNED_TILES = 2 * PASS // P
+DECAY_SLOTS = 6
 
 
 def tile_spectral_transmittance_channel_flux_h3_kernel(
@@ -65,503 +41,474 @@ def tile_spectral_transmittance_channel_flux_h3_kernel(
     with ExitStack() as ctx:
         keep = ctx.enter_context(tc.tile_pool(name="keep", bufs=1))
         work = ctx.enter_context(tc.tile_pool(name="work", bufs=3))
-        psum = ctx.enter_context(tc.psum_pool(name="psum", bufs=BANKS))
-        if MANUAL:
-            ctx.enter_context(tc.manual_schedule())
+        psum = ctx.enter_context(tc.psum_pool(name="psum", bufs=ROTATING_BANKS))
+        ctx.enter_context(tc.manual_schedule())
 
-        units = list(UNITS)
-        shadowed = list(SHADOWED)
-        row_units = [u for u, kind in zip(units, KINDS) if kind == "r"]
-        row_groups = sorted({cg for cg, q in row_units})
+        def span(index, width):
+            return slice(index * width, (index + 1) * width)
 
         def bank(shape, name):
             return psum.tile(shape, F32, name=name, tag="bank")
 
-        raw = {}
-
-        def load_profiles(q):
-            raw["p", q] = keep.tile([P, 2, A], BF16, name="raw_p%d" % q)
-            nc.sync.dma_start(out=raw["p", q][:], in_=profiles[256 * q : 256 * q + 256, :].rearrange("(t m) k -> m t k", t=2))
-
-        def load_absorption(g):
-            raw["a", g] = keep.tile([P, 4, A], BF16, name="raw_a%d" % g, tag="big", bufs=16)
-            nc.sync.dma_start(out=raw["a", g][:], in_=absorption[512 * g : 512 * g + 512, :].rearrange("(m t) k -> m t k", t=4))
-
-        def load_contrast(g, cg):
-            raw["c", g, cg] = keep.tile([P, 4, 512], BF16, name="raw_c%d_%d" % (g, cg), tag="big", bufs=16)
-            nc.sync.dma_start(
-                out=raw["c", g, cg][:],
-                in_=contrast[512 * g : 512 * g + 512, 512 * cg : 512 * cg + 512].rearrange("(p t) c -> p t c", t=4),
-            )
-
-        ident = keep.tile([P, P], F32, name="ident")
-        make_identity(nc, ident[:])
-        rows32 = keep.tile([P, P], F32, name="rows32")
-        nc.gpsimd.memset(rows32[:], 0.0)
-        weights = keep.tile([P, G, 4], BF16, name="weights")
-        rows16 = keep.tile([32, P], BF16, name="rows16")
-        cols = keep.tile([P, 32], F32, name="cols")
-        shift = keep.tile([P, 12], F32, name="shift")
-        spread = {}
-        wide = keep.tile([P, P], F32, name="wide")
-        wide_t = keep.tile([P, P], F32, name="wide_t")
-        nc.gpsimd.memset(wide[:], 0.0)
-        held_weights = psum.tile([P, P], F32, name="held_weights", bufs=1)
-
-        if HEAD == 1:
-            load_contrast(0, 0)
-        load_profiles(0)
-        if HEAD == 2:
-            load_contrast(0, 0)
-        load_absorption(0)
-        nc.sync.dma_start(out=weights[:], in_=band_weights.rearrange("(g p t) -> p g t", g=G, t=4))
-        for g in range(G):
-            if g > 0 or HEAD == 0:
-                load_contrast(g, 0)
-            if g + 1 < G:
-                load_absorption(g + 1)
-        nc.sync.dma_start(out=rows16[0:12, :], in_=gain.rearrange("(r i) -> r i", i=P))
-        nc.sync.dma_start(out=rows16[12:24, :], in_=offset.rearrange("(r i) -> r i", i=P))
-        nc.sync.dma_start(out=rows16[24:32, :], in_=angle_factor.rearrange("(r i) -> r i", i=P))
-        load_profiles(1)
-        load_contrast(0, 1)
-        load_profiles(2)
-        for g in range(1, G):
-            load_contrast(g, 1)
-        load_profiles(3)
-        for g in range(G):
-            load_contrast(g, 2)
-        lo, hi = 512 * row_groups[0], 512 * row_groups[-1] + 512
-        for name, vec in (("gain", gain), ("offset", offset)):
-            spread[name] = keep.tile([P, hi - lo], BF16, name="spread_" + name)
-            nc.sync.dma_start(out=spread[name][:], in_=vec[lo:hi].partition_broadcast(P))
-
-        p_codes = keep.tile([P, J], U32, name="p_codes", align_bytes=64)
-        p_scales = keep.tile([P, J], U8, name="p_scales", align_bytes=64)
-        a_codes, a_scales, h_codes, h_scales, c_codes, c_scales = {}, {}, {}, {}, {}, {}
-        for g in range(G):
-            a_codes[g] = keep.tile([P, 512], U32, name="a_codes%d" % g, align_bytes=64)
-            a_scales[g] = keep.tile([P, 512], U8, name="a_scales%d" % g, align_bytes=64)
-            h_codes[g] = keep.tile([P, J], U32, name="h_codes%d" % g, align_bytes=64)
-            h_scales[g] = keep.tile([P, J], U8, name="h_scales%d" % g, align_bytes=64)
-            c_codes[g] = keep.tile([P, B], U32, name="c_codes%d" % g, align_bytes=64)
-            c_scales[g] = keep.tile([P, B], U8, name="c_scales%d" % g, align_bytes=64)
-        y_scales = keep.tile([P, J], U8, name="y_scales", align_bytes=64)
-
         def quantize(codes, scales, grouped):
             nc.vector.quantize_mx(out=codes.bitcast(FP8X4), scales=scales, in_=grouped)
 
-        def matmul(out, lhs, lhs_scale, rhs, rhs_scale, start, stop):
+        def matmul(out, lhs, rhs, start, stop):
             nc.tensor.matmul_mx(
-                out=out, lhsT=lhs.bitcast(FP8X4), lhsT_scale=lhs_scale, rhs=rhs.bitcast(FP8X4), rhs_scale=rhs_scale,
+                out=out, lhsT=lhs[0].bitcast(FP8X4), lhsT_scale=lhs[1], rhs=rhs[0].bitcast(FP8X4), rhs_scale=rhs[1],
                 start=start, stop=stop,
             )
 
+        def packed(name, width):
+            codes = keep.tile([P, width], U32, name=name + "_codes", align_bytes=64)
+            scales = keep.tile([P, width], U8, name=name + "_scales", align_bytes=64)
+            return lambda columns: (codes[:, columns], scales[:, columns])
+
+        ident = keep.tile([P, P], F32, name="ident")
+        make_identity(nc, ident[:])
+        factor_rows = keep.tile([P, P], F32, name="factor_rows")
+        nc.gpsimd.memset(factor_rows[:], 0.0)
+        weights_wide = keep.tile([P, P], F32, name="weights_wide")
+        nc.gpsimd.memset(weights_wide[:], 0.0)
+        weights_turned = keep.tile([P, P], F32, name="weights_turned")
+        weights_raw = keep.tile([P, GROUPS, 4], BF16, name="weights_raw")
+        weights_psum = psum.tile([P, P], F32, name="weights_psum", bufs=1)
+        gain_at, offset_at, angle_at = 0, TURNED_TILES, 2 * TURNED_TILES
+        factor_count = angle_at + PROFILE_TILES
+        factor_raw = keep.tile([factor_count, P], BF16, name="factor_raw")
+        factors = keep.tile([P, factor_count], F32, name="factors")
+        shift = keep.tile([P, TURNED_TILES], F32, name="shift")
+        raw = {}
+
+        def load_profiles(q):
+            raw["profiles", q] = keep.tile([P, 2, LAYERS], BF16, name="raw_profiles%d" % q)
+            rows = profiles[span(q, QUARTER), :]
+            nc.sync.dma_start(out=raw["profiles", q][:], in_=rows.rearrange("(t m) k -> m t k", t=2))
+
+        def load_absorption(g):
+            raw["absorption", g] = keep.tile([P, 4, LAYERS], BF16, name="raw_absorption", tag="load", bufs=LOAD_SLOTS)
+            rows = absorption[span(g, PASS), :]
+            nc.sync.dma_start(out=raw["absorption", g][:], in_=rows.rearrange("(m t) k -> m t k", t=4))
+
+        def load_contrast(g, c):
+            raw["contrast", g, c] = keep.tile([P, 4, PASS], BF16, name="raw_contrast", tag="load", bufs=LOAD_SLOTS)
+            piece = contrast[span(g, PASS), span(c, PASS)]
+            nc.sync.dma_start(out=raw["contrast", g, c][:], in_=piece.rearrange("(p t) n -> p t n", t=4))
+
+        load_profiles(0)
+        for g in range(GROUPS):
+            load_absorption(g)
+            if g == 0:
+                nc.sync.dma_start(out=weights_raw[:], in_=band_weights.rearrange("(g p t) -> p g t", g=GROUPS, t=4))
+            load_contrast(g, 0)
+        for vector_in, at, count in ((gain, gain_at, TURNED_TILES), (offset, offset_at, TURNED_TILES), (angle_factor, angle_at, PROFILE_TILES)):
+            nc.sync.dma_start(out=factor_raw[at : at + count, :], in_=vector_in[: count * P].rearrange("(r i) -> r i", i=P))
+        load_profiles(1)
+        load_contrast(0, 1)
+        load_profiles(2)
+        for g in range(1, GROUPS):
+            load_contrast(g, 1)
+        load_profiles(3)
+        for g in range(GROUPS):
+            load_contrast(g, 2)
+        gain_spread = keep.tile([P, CHANNELS], BF16, name="gain_spread")
+        nc.sync.dma_start(out=gain_spread[:], in_=gain.partition_broadcast(P))
+        offset_spread = keep.tile([P, CHANNELS], BF16, name="offset_spread")
+        nc.sync.dma_start(out=offset_spread[:], in_=offset.partition_broadcast(P))
+
+        profiles_mx = packed("profiles", PROFILES)
+        absorption_mx = [packed("absorption%d" % g, PASS) for g in range(GROUPS)]
+        h_mx = [packed("h%d" % g, PROFILES) for g in range(GROUPS)]
+        contrast_mx = [packed("contrast%d" % g, CHANNELS) for g in range(GROUPS)]
+        y_scales = keep.tile([P, PROFILES], U8, name="y_scales", align_bytes=64)
+
+        steps = {}
         live = {}
 
-        def turn_item(key, slots, codes, scales):
+        def chain(names, calls, needs):
+            for name, call in zip(names, calls):
+                steps[name] = (list(needs), call)
+                needs = [name]
+
+        def words_to_partitions(source, tiles, name):
+            turned = bank([P, len(tiles), 2, P], name)
+            for t, tile in enumerate(tiles):
+                for u in range(2):
+                    nc.tensor.transpose(turned[:, t, u, :], source(tile, u), ident[:])
+            return turned
+
+        def words_out(grouped, turned):
+            nc.scalar.copy(
+                out=grouped.bitcast(F32).rearrange("p (t m u) -> p t m u", m=P, u=2),
+                in_=turned[:].rearrange("p t u m -> p t m u"),
+            )
+
+        def input_steps(kind, index, tiles, target):
+            key = (kind, index)
+
             def turn():
-                for pair in range(slots // 2):
-                    live[key, pair] = bank([P, 2, 2, P], "turned")
-                    for t in range(2):
-                        words = raw[key][:, 2 * pair + t, :].bitcast(F32)
-                        for u in range(2):
-                            nc.tensor.transpose(live[key, pair][:, t, u, :], words[:, u:256:2], ident[:])
+                for pair in range(tiles // 2):
+                    live[key, pair] = words_to_partitions(
+                        lambda t, u: raw[key][:, t, :].bitcast(F32)[:, u : LAYERS // 2 : 2],
+                        [2 * pair, 2 * pair + 1], "turned_input",
+                    )
 
             def leave():
-                live[key] = work.tile([P, slots * 512], BF16, name="grouped", tag="grouped", align_bytes=64)
-                for pair in range(slots // 2):
-                    words = live[key][:].bitcast(F32)[:, 512 * pair : 512 * pair + 512]
-                    nc.scalar.copy(
-                        out=words.rearrange("p (t m u) -> p t m u", t=2, u=2),
-                        in_=live[key, pair][:].rearrange("p t u m -> p t m u"),
-                    )
+                live[key] = work.tile([P, tiles * PASS], BF16, name="grouped", align_bytes=64)
+                for pair in range(tiles // 2):
+                    words_out(live[key][:, span(pair, 2 * PASS)], live[key, pair])
 
             def pack():
-                quantize(codes, scales, live[key][:])
+                quantize(*target, live[key][:])
 
-            return [], [("tr", turn), ("str", leave), ("v", pack)], key
+            chain([("turn",) + key, ("leave",) + key, ("pack",) + key], [turn, leave, pack], [])
 
-        def constants_item():
+        def weights_steps():
             def widen():
-                nc.vector.tensor_copy(out=rows32[0:32, :], in_=rows16[:])
+                nc.vector.tensor_copy(out=weights_wide[:, : 4 * GROUPS], in_=weights_raw[:].rearrange("p g t -> p (g t)"))
 
             def turn():
-                live["k"] = bank([P, P], "turned_rows")
-                nc.tensor.transpose(live["k"][:], rows32[:], ident[:])
+                live["weights"] = bank([P, P], "turned_weights")
+                nc.tensor.transpose(live["weights"][:], weights_wide[:], ident[:])
 
             def leave():
-                nc.scalar.copy(out=cols[:], in_=live["k"][:, 0:32])
+                nc.scalar.copy(out=weights_turned[:], in_=live["weights"][:])
+
+            def turn_back():
+                nc.tensor.transpose(weights_psum[:], weights_turned[:], ident[:])
+
+            names = [(verb, "weights") for verb in ("widen", "turn", "leave", "hold")]
+            chain(names, [widen, turn, leave, turn_back], [])
+
+        def factor_steps():
+            def widen():
+                nc.vector.tensor_copy(out=factor_rows[:factor_count, :], in_=factor_raw[:])
+
+            def turn():
+                live["factors"] = bank([P, P], "turned_factors")
+                nc.tensor.transpose(live["factors"][:], factor_rows[:], ident[:])
+
+            def leave():
+                nc.scalar.copy(out=factors[:], in_=live["factors"][:, :factor_count])
 
             def product():
-                nc.vector.tensor_tensor(out=shift[:], in0=cols[:, 0:12], in1=cols[:, 12:24], op=ALU.mult)
+                nc.vector.tensor_tensor(
+                    out=shift[:], in0=factors[:, gain_at:offset_at], in1=factors[:, offset_at:angle_at], op=ALU.mult
+                )
 
-            return [], [("v", widen), ("tr", turn), ("str", leave), ("v", product)], "k"
+            names = [(verb, "factors") for verb in ("widen", "turn", "leave", "shift")]
+            chain(names, [widen, turn, leave, product], [])
 
-        def weights_item():
-            def widen():
-                nc.vector.tensor_copy(out=wide[:, 0:16], in_=weights[:].rearrange("p g t -> p (g t)"))
+        def contrast_steps(g, c, shared, gate):
+            key = ("contrast", g, c)
+            split = GPSIMD_CHANNELS if shared else 0
 
-            def turn():
-                live["w1"] = bank([P, P], "turned_weights")
-                nc.tensor.transpose(live["w1"][:], wide[:], ident[:])
-
-            def leave():
-                nc.scalar.copy(out=wide_t[:], in_=live["w1"][:])
-
-            def back():
-                nc.tensor.transpose(held_weights[:], wide_t[:], ident[:])
-
-            return [], [("", widen), ("", turn), ("", leave), ("", back)], "w"
-
-        def contrast_item(g, cg):
-            key = ("c", g, cg)
-            shared = (g, cg) in shadowed
-            split = G_WIDTH if shared else 0
-
-            def tile():
-                if shared or (g, cg) in GATES:
-                    live[key] = work.tile([P, 2048], BF16, name="woven", bufs=1, align_bytes=64)
+            def allocate():
+                if shared or gate:
+                    live[key] = work.tile([P, 4 * PASS], BF16, name="grouped_shared", bufs=1, align_bytes=64)
                 else:
-                    live[key] = work.tile([P, 2048], BF16, name="grouped", tag="grouped", align_bytes=64)
+                    live[key] = work.tile([P, 4 * PASS], BF16, name="grouped", align_bytes=64)
 
             def weave_first():
-                tile()
-                if split:
-                    nc.gpsimd.tensor_scalar(
-                        out=live[key][:, : 4 * split].rearrange("p (c t) -> p c t", t=4),
-                        in0=raw[key][:, :, :split].rearrange("p t c -> p c t"),
-                        scalar1=1.0, scalar2=0.0, op0=ALU.mult, op1=ALU.add,
-                    )
+                allocate()
+                nc.gpsimd.tensor_scalar(
+                    out=live[key][:, : 4 * split].rearrange("p (n t) -> p n t", t=4),
+                    in0=raw[key][:, :, :split].rearrange("p t n -> p n t"),
+                    scalar1=1.0, scalar2=0.0, op0=ALU.mult, op1=ALU.add,
+                )
 
             def weave():
                 if not shared:
-                    tile()
-                copy = nc.scalar.copy if (g, cg) in SCALAR_PIECES else nc.vector.tensor_copy
-                if split < 512:
-                    copy(
-                        out=live[key][:, 4 * split :].rearrange("p (c i t) -> p c t i", i=4, t=4),
-                        in_=raw[key][:, :, split:].rearrange("p t (c i) -> p c t i", i=4),
-                    )
+                    allocate()
+                nc.vector.tensor_copy(
+                    out=live[key][:, 4 * split :].rearrange("p (n i t) -> p n t i", i=4, t=4),
+                    in_=raw[key][:, :, split:].rearrange("p t (n i) -> p n t i", i=4),
+                )
 
             def pack():
-                window = slice(512 * cg, 512 * cg + 512)
-                quantize(c_codes[g][:, window], c_scales[g][:, window], live[key][:])
+                quantize(*contrast_mx[g](span(c, PASS)), live[key][:])
 
-            return weave_first, weave, pack
+            if shared:
+                steps["weave_first", g, c] = ([], weave_first)
+            chain([("weave", g, c), ("pack", "contrast", g, c)], [weave, pack], [("weave_first", g, c)] if shared else [])
 
-        def transmittance_item(g, q):
+        def h_steps(g, q):
             key = ("h", g, q)
 
             def depth():
-                for jt in range(2):
-                    live[key, jt] = bank([P, 4, P], "tau")
-                    window = slice(256 * q + P * jt, 256 * q + P * jt + P)
+                for half in range(2):
+                    live[key, half] = bank([P, 4, P], "tau")
                     for t in range(4):
-                        slot = slice(P * t, P * t + P)
-                        matmul(live[key, jt][:, t, :], a_codes[g][:, slot], a_scales[g][:, slot],
-                               p_codes[:, window], p_scales[:, window], True, True)
+                        matmul(live[key, half][:, t, :], absorption_mx[g](span(t, P)),
+                               profiles_mx(span(2 * q + half, P)), True, True)
 
             def decay():
-                live[key, "e"] = work.tile([P, 256, 4], F32, name="decay", bufs=E_BUFS)
-                for jt in range(2):
+                live[key, "decay"] = work.tile([P, QUARTER, 4], F32, name="decay", bufs=DECAY_SLOTS)
+                for half in range(2):
                     nc.scalar.activation(
-                        out=live[key, "e"][:, P * jt : P * jt + P, :], in_=live[key, jt][:].rearrange("p t n -> p n t"),
+                        out=live[key, "decay"][:, span(half, P), :], in_=live[key, half][:].rearrange("p t n -> p n t"),
                         func=ACT.Exp, scale=-1.0,
                     )
 
             def weigh():
-                live[key] = work.tile([P, 256, 4], BF16, name="weighed", align_bytes=64)
+                live[key] = work.tile([P, QUARTER, 4], BF16, name="weighed", align_bytes=64)
                 nc.vector.tensor_tensor(
-                    out=live[key][:], in0=live[key, "e"][:], in1=held_weights[:, 4 * g : 4 * g + 4].unsqueeze(1).to_broadcast([P, 256, 4]),
-                    op=ALU.mult,
+                    out=live[key][:], in0=live[key, "decay"][:],
+                    in1=weights_psum[:, span(g, 4)].unsqueeze(1).to_broadcast([P, QUARTER, 4]), op=ALU.mult,
                 )
 
             def pack():
-                window = slice(256 * q, 256 * q + 256)
-                quantize(h_codes[g][:, window], h_scales[g][:, window], live[key][:].rearrange("p n t -> p (n t)"))
+                quantize(*h_mx[g](span(q, QUARTER)), live[key][:].rearrange("p n t -> p (n t)"))
 
-            first = [("a", g), ("p", q)], [("mm", depth), ("smm", decay)], ("e", g, q)
-            return first, ([("e", g, q)], [("v", weigh), ("v", pack)], key)
+            chain([("depth", g, q), ("decay", g, q)], [depth, decay], [("pack", "absorption", g), ("pack", "profiles", q)])
+            chain([("weigh", g, q), ("pack", "h", g, q)], [weigh, pack], [("decay", g, q), ("hold", "weights")])
 
-        def operands(cg, q, chs):
-            return []
+        def operands(c, q):
+            return [("pack", "h", g, q) for g in range(GROUPS)] + [("pack", "contrast", g, c) for g in range(GROUPS)]
 
-        def column_item(cg, q, half):
-            key = ("z", cg, q, half)
+        def new_y(patch):
+            live["y", patch] = keep.tile([P, 2, PASS], F32, name="y", tag="load", bufs=LOAD_SLOTS)
 
-            def product():
-                live[key] = bank([P, 2, 256], "flux_t")
-                window = slice(256 * q, 256 * q + 256)
+        def angle(q, half):
+            column = angle_at + 2 * q + half
+            return factors[:, column : column + 1]
+
+        def turned_patch_steps(patch, c, q):
+            def product(half):
+                live["flux", patch, half] = bank([P, 2, QUARTER], "flux_turned")
                 for i in range(2):
-                    ct = 4 * cg + 2 * half + i
-                    slot = slice(P * ct, P * ct + P)
-                    for g in range(G):
-                        matmul(live[key][:, i, :], c_codes[g][:, slot], c_scales[g][:, slot],
-                               h_codes[g][:, window], h_scales[g][:, window], g == 0, g == G - 1)
+                    for g in range(GROUPS):
+                        matmul(live["flux", patch, half][:, i, :], contrast_mx[g](span(4 * c + 2 * half + i, P)),
+                               h_mx[g](span(q, QUARTER)), g == 0, g == GROUPS - 1)
 
-            def leave():
+            def scale(half):
                 if half == 0:
-                    live["z", cg, q] = work.tile([P, 4, 256], F32, name="scaled", bufs=4)
+                    live["scaled", patch] = work.tile([P, 4, QUARTER], F32, name="scaled")
                 for i in range(2):
-                    ct = 4 * cg + 2 * half + i
+                    tile = 4 * c + 2 * half + i
                     nc.scalar.activation(
-                        out=live["z", cg, q][:, 2 * half + i, :], in_=live[key][:, i, :], func=ACT.Identity,
-                        scale=cols[:, ct : ct + 1], bias=shift[:, ct : ct + 1],
+                        out=live["scaled", patch][:, 2 * half + i, :], in_=live["flux", patch, half][:, i, :],
+                        func=ACT.Identity, scale=factors[:, gain_at + tile : gain_at + tile + 1], bias=shift[:, tile : tile + 1],
                     )
-
-            return operands(cg, q, [2 * cg + half]), [("mm", product), ("smm", leave)], key
-
-        def back_item(cg, q):
-            key = ("y", cg, q, 1)
 
             def turn():
-                for jt in range(2):
-                    live[key, jt] = bank([P, 4, P], "turned_back")
+                for half in range(2):
+                    live["back", patch, half] = bank([P, 4, P], "turned_back")
                     for i in range(4):
-                        nc.tensor.transpose(live[key, jt][:, i, :], live["z", cg, q][:, i, P * jt : P * jt + P], ident[:])
+                        nc.tensor.transpose(
+                            live["back", patch, half][:, i, :], live["scaled", patch][:, i, span(half, P)], ident[:]
+                        )
 
             def leave():
-                live["y", cg, q] = keep.tile([P, 2, 512], F32, name="y", tag="big", bufs=16)
-                for jt in range(2):
-                    col = 24 + 2 * q + jt
+                new_y(patch)
+                for half in range(2):
                     nc.scalar.activation(
-                        out=live["y", cg, q][:, jt, :], in_=live[key, jt][:].rearrange("p i c -> p (i c)"),
-                        func=ACT.Copy, scale=cols[:, col : col + 1],
+                        out=live["y", patch][:, half, :], in_=live["back", patch, half][:].rearrange("p i n -> p (i n)"),
+                        func=ACT.Copy, scale=angle(q, half),
                     )
 
-            return [("z", cg, q, 0), ("z", cg, q, 1)], [("tr", turn), ("str", leave)], key
+            for half in range(2):
+                chain([("product", patch, half), ("scale", patch, half)],
+                      [lambda half=half: product(half), lambda half=half: scale(half)],
+                      operands(c, q) + [("shift", "factors")])
+            chain([("turn", "back", patch), ("leave", "back", patch)], [turn, leave],
+                  [("scale", patch, 0), ("scale", patch, 1)])
+            return [("leave", "back", patch)]
 
-        def row_item(cg, q, jt):
-            key = ("y", cg, q, jt)
-            window = slice(512 * cg, 512 * cg + 512)
-            part = slice(512 * cg - lo, 512 * cg - lo + 512)
+        def straight_patch_steps(patch, c, q):
+            def product(half):
+                live["flux", patch, half] = bank([P, PASS], "flux")
+                for g in range(GROUPS):
+                    matmul(live["flux", patch, half][:], h_mx[g](span(2 * q + half, P)),
+                           contrast_mx[g](span(c, PASS)), g == 0, g == GROUPS - 1)
 
-            def product():
-                live[key] = bank([P, 512], "flux")
-                slot = slice(256 * q + P * jt, 256 * q + P * jt + P)
-                for g in range(G):
-                    matmul(live[key][:], h_codes[g][:, slot], h_scales[g][:, slot],
-                           c_codes[g][:, window], c_scales[g][:, window], g == 0, g == G - 1)
-
-            def shifted():
-                live[key, "t"] = work.tile([P, 512], F32, name="shifted")
-                nc.vector.tensor_tensor(out=live[key, "t"][:], in0=live[key][:], in1=spread["offset"][:, part], op=ALU.add)
-
-            def scaled():
-                if jt == 0:
-                    live["y", cg, q] = keep.tile([P, 2, 512], F32, name="y", tag="big", bufs=16)
-                col = 24 + 2 * q + jt
-                nc.vector.scalar_tensor_tensor(
-                    out=live["y", cg, q][:, jt, :], in0=live[key, "t"][:], scalar=cols[:, col : col + 1],
-                    in1=spread["gain"][:, part], op0=ALU.mult, op1=ALU.mult,
+            def add(half):
+                live["sum", patch, half] = work.tile([P, PASS], F32, name="summed")
+                nc.vector.tensor_tensor(
+                    out=live["sum", patch, half][:], in0=live["flux", patch, half][:],
+                    in1=offset_spread[:, span(c, PASS)], op=ALU.add,
                 )
 
-            return operands(cg, q, [2 * cg, 2 * cg + 1]), [("mm", product), ("v", shifted), ("v", scaled)], key
+            def finish(half):
+                if half == 0:
+                    new_y(patch)
+                nc.vector.scalar_tensor_tensor(
+                    out=live["y", patch][:, half, :], in0=live["sum", patch, half][:], scalar=angle(q, half),
+                    in1=gain_spread[:, span(c, PASS)], op0=ALU.mult, op1=ALU.mult,
+                )
 
-        def planes_item(cg, q, first, count, by_scalar):
-            key = ("w", cg, q, first)
-            window = slice(256 * q + P * first, 256 * q + P * (first + count))
+            for half in range(2):
+                chain([("product", patch, half), ("add", patch, half), ("finish", patch, half)],
+                      [lambda half=half: product(half), lambda half=half: add(half), lambda half=half: finish(half)],
+                      operands(c, q))
+            return [("finish", patch, 0), ("finish", patch, 1)]
+
+        def output_steps(part, c, q, first, count, done):
+            patch = min(part, PATCHES - 1)
             tiles = slice(first, first + count)
+            rows = slice(q * QUARTER + first * P, q * QUARTER + (first + count) * P)
 
             def store_y():
                 nc.sync.dma_start(
-                    out=out_0[window, 512 * cg : 512 * cg + 512].rearrange("(t p) c -> p t c", t=count),
-                    in_=live["y", cg, q][:, tiles, :],
+                    out=out_0[rows, span(c, PASS)].rearrange("(t p) n -> p t n", t=count), in_=live["y", patch][:, tiles, :]
                 )
 
             def round_y():
-                live[key, "b"] = work.tile([P, 512 * count], BF16, name="rounded", bufs=R_BUFS)
-                cast = nc.scalar.copy if by_scalar else nc.vector.tensor_copy
-                cast(
-                    out=live[key, "b"][:].rearrange("p (t u m e) -> p t u m e", t=count, u=2, e=2),
-                    in_=live["y", cg, q][:, tiles, :].rearrange("p t (m u e) -> p t u m e", u=2, e=2),
+                live["rounded", part] = work.tile([P, count * PASS], BF16, name="rounded", bufs=4)
+                copy = nc.vector.tensor_copy if patch == PATCHES - 1 else nc.scalar.copy
+                copy(
+                    out=live["rounded", part][:].rearrange("p (t u m e) -> p t u m e", t=count, u=2, e=2),
+                    in_=live["y", patch][:, tiles, :].rearrange("p t (m u e) -> p t u m e", u=2, e=2),
                 )
 
             def turn():
-                live[key] = bank([P, count, 2, P], "turned_y")
-                words = live[key, "b"][:].bitcast(F32)
-                for t in range(count):
-                    for u in range(2):
-                        at = 256 * t + P * u
-                        nc.tensor.transpose(live[key][:, t, u, :], words[:, at : at + P], ident[:])
+                words = live["rounded", part][:].bitcast(F32)
+                live["planes", part] = words_to_partitions(lambda t, u: words[:, span(2 * t + u, P)], range(count), "turned_y")
 
             def leave():
-                live[key, "g"] = work.tile([P, 512 * count], BF16, name="grouped_y", bufs=R_BUFS, align_bytes=64)
-                nc.scalar.copy(
-                    out=live[key, "g"][:].bitcast(F32).rearrange("p (t m u) -> p t m u", t=count, u=2),
-                    in_=live[key][:].rearrange("p t u m -> p t m u"),
-                )
+                live["grouped", part] = work.tile([P, count * PASS], BF16, name="grouped_y", bufs=4, align_bytes=64)
+                words_out(live["grouped", part][:], live["planes", part])
 
             def pack():
-                live[key, "c"] = work.tile([P, P * count], U32, name="y_codes", bufs=R_BUFS, align_bytes=64)
-                quantize(live[key, "c"][:], y_scales[4 * cg : P, window], live[key, "g"][:])
+                if first == 0:
+                    live["codes", patch] = work.tile([P, QUARTER], U32, name="y_codes", bufs=4, align_bytes=64)
+                codes = live["codes", patch][:, first * P : (first + count) * P]
+                quantize(codes, y_scales[4 * c : P, rows], live["grouped", part][:])
 
-            def store():
-                words = out_1[cg].rearrange("p m t -> p (m t)").bitcast(I32)
-                nc.sync.dma_start(out=words[:, window], in_=live[key, "c"][:].bitcast(I32))
+            def store_codes():
+                words = out_1[c].rearrange("p m t -> p (m t)").bitcast(I32)
+                nc.sync.dma_start(out=words[:, span(q, QUARTER)], in_=live["codes", patch][:].bitcast(I32))
 
-            return [round_y, turn, leave, pack, store, store_y]
+            steps["store", "y", part] = (done, store_y)
+            chain([("round", part), ("turn", "y", part), ("leave", "y", part), ("pack", "y", part)],
+                  [round_y, turn, leave, pack], done)
+            if first + count == 2:
+                steps["store", "codes", patch] = ([("pack", "y", part)], store_codes)
 
-        ops = {}
+        pairs = [(g, q) for q in range(QUARTERS) for g in range(0, GROUPS, 2)]
+        last = GROUPS - 1
+        shared_pieces = [(last, 0)] + [(g, 1) for g in range(last)] + [(g, 2) for g in range(GROUPS)]
+        weights_steps()
+        factor_steps()
+        for q in range(QUARTERS):
+            input_steps("profiles", q, 2, profiles_mx(span(q, QUARTER)))
+        for g in range(GROUPS):
+            input_steps("absorption", g, 4, absorption_mx[g](span(0, PASS)))
+            for c in range(THIRDS):
+                contrast_steps(g, c, (g, c) in shared_pieces, (g, c) == (last - 1, 0))
+            for q in range(QUARTERS):
+                h_steps(g, q)
 
-        def chain(names, item, extra):
-            needs, stages, key = item
-            before = list(extra)
-            for name, (tag, call) in zip(names, stages):
-                ops[name] = (before, call)
-                before = [name]
+        vector = [("widen", "weights"), ("pack", "profiles", 0)]
+        for g in range(last):
+            vector.extend([("weave", g, 0), ("pack", "absorption", g), ("pack", "contrast", g, 0)])
+        gpsimd = []
+        for i, ((g, q), piece) in enumerate(zip(pairs, shared_pieces)):
+            gpsimd.append(("weave_first",) + piece)
+            steps[gpsimd[-1]][0].append(vector[-1])
+            vector.extend([("weigh", g, q), ("weigh", g + 1, q), ("weave",) + piece])
+            if i == 0:
+                vector.append(("pack", "absorption", last))
+            vector.extend([("pack", "h", g, q), ("pack", "h", g + 1, q)])
+            if i == 0:
+                vector.extend([("widen", "factors"), ("pack", "profiles", 1)])
+            if i == 1:
+                vector.extend([("shift", "factors"), ("pack", "profiles", 2)])
+            if i == 3:
+                vector.extend([("weave", last, 1), ("pack", "profiles", 3), ("pack", "contrast", last, 1)])
+            vector.append(("pack", "contrast") + piece)
 
-        def held(cg, q, chs):
-            return [("qh", g, q) for g in range(G)] + [("qc", g, cg) for g in range(G)] + [("k", 3)]
-
-        for q in range(NQ):
-            window = slice(256 * q, 256 * q + 256)
-            chain([(n, q) for n in ("tp", "xp", "qp")], turn_item(("p", q), 2, p_codes[:, window], p_scales[:, window]), [])
-        for g in range(G):
-            chain([(n, g) for n in ("ta", "xa", "qa")], turn_item(("a", g), 4, a_codes[g][:], a_scales[g][:]), [])
-            for cg in range(NC):
-                first, weave, pack = contrast_item(g, cg)
-                if (g, cg) in shadowed:
-                    ops["g", g, cg] = ([], first)
-                ops["w", g, cg] = ([("g", g, cg)] if (g, cg) in shadowed else [], weave)
-                ops["qc", g, cg] = ([("w", g, cg)], pack)
-            for q in range(NQ):
-                first, second = transmittance_item(g, q)
-                chain([("d", g, q), ("e", g, q)], first, [("qa", g), ("qp", q)])
-                chain([("m", g, q), ("qh", g, q)], second, [("e", g, q)])
-        chain([("k", i) for i in range(4)], constants_item(), [])
-        chain([("j", i) for i in range(4)], weights_item(), [])
-        for g in range(G):
-            for q in range(NQ):
-                ops["m", g, q][0].append(("j", 3))
-        for u, (cg, q) in enumerate(units):
-            if (cg, q) in row_units:
-                for jt in range(2):
-                    chain([("z", u, jt), ("rs", u, jt), ("ry", u, jt)], row_item(cg, q, jt), held(cg, q, [2 * cg, 2 * cg + 1]))
-                done = [("ry", u, 0), ("ry", u, 1)]
+        patches = sorted(
+            ((c, q) for c in range(THIRDS) for q in range(QUARTERS)),
+            key=lambda cq: max(vector.index(name) for name in operands(*cq)),
+        )
+        for patch, (c, q) in enumerate(patches):
+            kind = turned_patch_steps if patch < TURNED_PATCHES else straight_patch_steps
+            done = kind(patch, c, q)
+            if patch < PATCHES - 1:
+                output_steps(patch, c, q, 0, 2, done)
             else:
-                for half in range(2):
-                    chain([("z", u, half), ("zx", u, half)], column_item(cg, q, half), held(cg, q, [2 * cg + half]))
-                chain([("b", u), ("bx", u)], back_item(cg, q), [("zx", u, 0), ("zx", u, 1)])
-                done = [("bx", u)]
-            pieces = [(u, 0, 2, done)] if u + 1 < len(units) else [(u, 0, 1, done[:1]), (u + 1, 1, 1, done[1:])]
-            for part, first, count, needs in pieces:
-                stages = planes_item(cg, q, first, count, CAST_S[part] == "1")
-                chain([(n, part) for n in ("c", "tw", "xw", "qy", "sw")], ([], [("", s) for s in stages[:5]], 0), needs)
-                ops["sy", part] = (needs, stages[5])
+                output_steps(patch, c, q, 0, 1, done[:1])
+                output_steps(patch + 1, c, q, 1, 1, done[1:])
+        parts = PATCHES + 1
 
-        rows = [u for u in range(len(units)) if units[u] in row_units]
-        parts = len(units) + 1
-        by_scalar = [u for u in range(parts) if CAST_S[u] == "1"]
-
-        tensor = list(TENSOR_FRONT)
-        depths = [("d", g, q) for q in range(1, NQ) for g in range(G)]
-        at = 0
-        rounds = max(TW_ROUND) + 1
-        ends = []
+        tensor = [("turn", "profiles", 0), ("turn", "absorption", 0), ("turn", "weights")]
+        for g in range(GROUPS):
+            if g < last:
+                tensor.append(("turn", "absorption", g + 1))
+            if g == 0:
+                tensor.append(("hold", "weights"))
+            if g >= 2:
+                tensor.append(("turn", "profiles", g - 1))
+            tensor.append(("depth", g, 0))
+        tensor.append(("turn", "factors"))
+        depth_round = {(g, q): q - 1 if q < 3 else 2 + g // 2 for g in range(GROUPS) for q in range(1, QUARTERS)}
+        planes_round = [max(FIRST_PLANES_ROUND + part // 2, min(part, PATCHES - 1) + 2) for part in range(parts)]
+        rounds = planes_round[-1] + 1
+        round_ends = []
         for r in range(rounds):
-            count = D_PER_ROUND[r] if r < len(D_PER_ROUND) else 0
-            turns = []
-            if 1 <= r <= len(units) and r - 1 not in rows:
-                turns.append(("b", r - 1))
-            turns.extend(("tw", u) for u in range(parts) if TW_ROUND[u] == r)
-            for q in range(2, NQ):
-                if r == P_ROUND[q - 2]:
-                    turns.append(("tp", q))
-            mms = depths[at : at + count]
-            at = at + count
-            product = [("z", r, 0), ("z", r, 1)] if r < len(units) else []
-            if r in EARLY_TURN:
-                tensor.extend(mms + turns + product)
-            else:
-                tensor.extend(mms + product + turns)
-            ends.append(tensor[-1])
+            depths = [("depth", g, q) for (g, q) in sorted(depth_round) if depth_round[g, q] == r]
+            products = [("product", r, half) for half in range(2)] if r < PATCHES else []
+            turns = [("turn", "back", r - 1)] if 1 <= r <= TURNED_PATCHES else []
+            turns.extend(("turn", "y", part) for part in range(parts) if planes_round[part] == r)
+            if r == 0:
+                turns.append(("turn", "profiles", 3))
+            tensor.extend(depths + turns + products if r == 1 else depths + products + turns)
+            round_ends.append(tensor[-1])
 
-        exits = {"tp": "xp", "ta": "xa", "d": "e", "z": "zx", "b": "bx", "tw": "xw"}
+        def emptied_by(name):
+            if name[0] == "turn":
+                return ("leave",) + name[1:]
+            if name[0] == "depth":
+                return ("decay",) + name[1:]
+            return ("scale" if name[1] < TURNED_PATCHES else "add",) + name[1:]
+
+        fills = [name for name in tensor if name[0] != "hold"]
         scalar = []
-        for name in tensor:
-            if name[0] in "kj":
-                if name[1] == 1:
-                    scalar.append((name[0], 2))
-            elif name[0] != "z" or name[1] not in rows:
-                scalar.append((exits[name[0]],) + name[1:])
-            for g, ch, after in SCALAR_AT:
-                if name == after:
-                    scalar.append(("w", g, ch))
-            if name in ends:
-                scalar.extend(("c", u) for u in by_scalar if TW_ROUND[u] == ends.index(name) + CS_BACK)
-
-        vector = list(FRONT_ORDER)
-        pairs = [(g, q) for q in range(NQ) for g in range(0, G, 2)]
-        for i, (g, q) in enumerate(pairs):
-            vector.extend([("m", g, q), ("m", g + 1, q)])
-            piece = shadowed[i]
-            ops[("g",) + piece][0].append(vector[-3])
-            extra = AFTER_PAIR.get(i, [])
-            vector.extend([("w",) + piece] + extra[:1] + [("qh", g, q), ("qh", g + 1, q)] + extra[1:])
-            vector.append(("qc",) + piece)
-            vector.extend(GATE_AFTER.get(i, []))
-        gpsimd = [("g",) + piece for piece in shadowed]
-        last = len(units) - 1
-        for r in range(rounds + 1):
-            casts = [("c", u) for u in range(parts) if TW_ROUND[u] == r + 1 and u not in by_scalar]
-            packs = [("qy", u) for u in range(parts) if TW_ROUND[u] == r - Q_LAG]
-            if r == rounds:
-                packs = [("qy", u) for u in range(parts) if TW_ROUND[u] >= r - Q_LAG]
-            line = [("ry", r - 1, 1)] if r - 1 in rows and LATE_RY and r - 1 < last else []
-            early = [c for c in casts if c[1] < r - 1 or not line]
-            late = [c for c in casts if c not in early]
-            if r == last:
-                line = line + packs + [("rs", r, 0), ("rs", r, 1), ("ry", r, 0)] + [c for c in casts if c[1] < r] + [("ry", r, 1)] + [c for c in casts if c[1] >= r]
-            elif r in rows and LATE_RY:
-                line = line + early[:1] + [("rs", r, 0)] + packs[:1] + [("rs", r, 1)] + packs[1:] + [("ry", r, 0)] + early[1:] + late
-            elif r in rows:
-                line = early[:1] + [("rs", r, 0)] + packs[:1] + [("rs", r, 1), ("ry", r, 0)] + packs[1:] + [("ry", r, 1)] + early[1:]
-            else:
-                line = line + casts + packs
-            vector.extend(name for name in line if name not in vector)
+        for name in fills:
+            if emptied_by(name)[0] != "add":
+                scalar.append(emptied_by(name))
+            if name in round_ends:
+                ahead = round_ends.index(name) + 2
+                scalar.extend(("round", patch) for patch in range(PATCHES - 1) if planes_round[patch] == ahead)
 
         stores = []
         for r in range(rounds + 1):
-            stores.extend(("sw", u) for u in range(parts) if TW_ROUND[u] == r - 1 - Q_LAG)
-            if 1 <= r <= parts:
-                stores.append(("sy", r - 1))
-        stores.extend(("sw", u) for u in range(parts) if ("sw", u) not in stores)
-
-        banks = []
-        for name in tensor:
-            if name[0] == "z" and name[1] in rows:
-                free = ("rs",) + name[1:]
-            elif name == ("j", 3):
-                continue
-            elif name[0] in "kj":
-                free = (name[0], 2)
+            packs = [("pack", "y", part) for part in range(parts) if planes_round[part] == r - 1]
+            if TURNED_PATCHES <= r < PATCHES:
+                vector.extend([("add", r, 0)] + packs[:1] + [("add", r, 1), ("finish", r, 0)] + packs[1:] + [("finish", r, 1)])
             else:
-                free = (exits[name[0]],) + name[1:]
-            count = 2 if name[0] in ("ta", "d", "b") else 1
-            ops[name][0].extend(banks[i] for i in range(len(banks) - BANKS, len(banks) - BANKS + count) if i >= 0)
-            banks.extend([free] * count)
-        decays = [name for name in scalar if name[0] == "e"]
-        for i in range(E_BUFS, len(decays)):
-            ops[decays[i]][0].append(("m",) + decays[i - E_BUFS][1:])
+                vector.extend(packs)
+            if r == PATCHES - 1:
+                vector.extend([("round", r), ("round", r + 1)])
+            stores.extend(("store", "codes", patch) for patch in range(PATCHES) if planes_round[patch] == r - 2)
+            if 1 <= r <= parts:
+                stores.append(("store", "y", r - 1))
+        stores.append(("store", "codes", PATCHES - 1))
+
+        filled = []
+        for name in fills:
+            banks = 2 if name[0] == "depth" or name[:2] in (("turn", "absorption"), ("turn", "back")) else 1
+            first = len(filled) - ROTATING_BANKS
+            steps[name][0].extend(filled[i] for i in range(max(first, 0), max(first + banks, 0)))
+            filled.extend([emptied_by(name)] * banks)
+        decays = [name for name in scalar if name[0] == "decay"]
+        for earlier, later in zip(decays, decays[DECAY_SLOTS:]):
+            steps[later][0].append(("weigh",) + earlier[1:])
 
         programs = [gpsimd, vector, scalar, tensor, stores]
         heads = [0] * len(programs)
         written = set()
-        while any(heads[i] < len(program) for i, program in enumerate(programs)):
-            moved = False
+        while any(head < len(program) for head, program in zip(heads, programs)):
             for i, program in enumerate(programs):
-                while heads[i] < len(program) and all(n in written for n in ops[program[heads[i]]][0]):
-                    ops[program[heads[i]]][1]()
+                while heads[i] < len(program) and all(name in written for name in steps[program[heads[i]]][0]):
+                    steps[program[heads[i]]][1]()
                     written.add(program[heads[i]])
                     heads[i] = heads[i] + 1
-                    moved = True
-            assert moved, [program[heads[i] : heads[i] + 1] for i, program in enumerate(programs)]
 
         scale_rows = out_2.bitcast(I32)
         for quadrant in range(4):
             nc.scalar.dma_start(
-                out=scale_rows[:, 4 * quadrant : 4 * quadrant + 4, :],
-                in_=y_scales[32 * quadrant : 32 * quadrant + 4 * NC, :].bitcast(I32),
+                out=scale_rows[:, span(quadrant, 4), :],
+                in_=y_scales[32 * quadrant : 32 * quadrant + 4 * THIRDS, :].bitcast(I32),
             )

@@ -25,7 +25,8 @@ PATCHES = THIRDS * QUARTERS
 CHANNEL_TILES = CHANNELS // P
 PROFILE_TILES = PROFILES // P
 
-GPSIMD_CHANNELS = 344
+SHARE_OF_TWO = 344
+SHARE_AFTER_WHOLE = 272
 TURNED_PATCHES = 5
 FIRST_PLANES_ROUND = 6
 ROTATING_BANKS = 7
@@ -199,38 +200,39 @@ def tile_spectral_transmittance_channel_flux_h3_kernel(
             names = [(verb, "factors") for verb in ("widen", "turn", "leave", "shift")]
             chain(names, [widen, turn, leave, product], [])
 
-        def contrast_steps(g, c, shared, gate):
+        def contrast_steps(g, c, share, paced):
             key = ("contrast", g, c)
-            split = GPSIMD_CHANNELS if shared else 0
 
             def allocate():
-                if shared or gate:
-                    live[key] = work.tile([P, 4 * PASS], BF16, name="grouped_shared", bufs=1, align_bytes=64)
+                if paced:
+                    live[key] = work.tile([P, 4 * PASS], BF16, name="grouped_paced", bufs=1, align_bytes=64)
                 else:
                     live[key] = work.tile([P, 4 * PASS], BF16, name="grouped", align_bytes=64)
 
-            def weave_first():
+            def weave_share():
                 allocate()
                 nc.gpsimd.tensor_scalar(
-                    out=live[key][:, : 4 * split].rearrange("p (n t) -> p n t", t=4),
-                    in0=raw[key][:, :, :split].rearrange("p t n -> p n t"),
+                    out=live[key][:, : 4 * share].rearrange("p (n t) -> p n t", t=4),
+                    in0=raw[key][:, :, :share].rearrange("p t n -> p n t"),
                     scalar1=1.0, scalar2=0.0, op0=ALU.mult, op1=ALU.add,
                 )
 
             def weave():
-                if not shared:
+                if share == 0:
                     allocate()
                 nc.vector.tensor_copy(
-                    out=live[key][:, 4 * split :].rearrange("p (n i t) -> p n t i", i=4, t=4),
-                    in_=raw[key][:, :, split:].rearrange("p t (n i) -> p n t i", i=4),
+                    out=live[key][:, 4 * share :].rearrange("p (n i t) -> p n t i", i=4, t=4),
+                    in_=raw[key][:, :, share:].rearrange("p t (n i) -> p n t i", i=4),
                 )
 
             def pack():
                 quantize(*contrast_mx[g](span(c, PASS)), live[key][:])
 
-            if shared:
-                steps["weave_first", g, c] = ([], weave_first)
-            chain([("weave", g, c), ("pack", "contrast", g, c)], [weave, pack], [("weave_first", g, c)] if shared else [])
+            stages = [(("weave_share", g, c), weave_share)] if share > 0 else []
+            if share < PASS:
+                stages.append((("weave", g, c), weave))
+            stages.append((("pack", "contrast", g, c), pack))
+            chain([name for name, call in stages], [call for name, call in stages], [])
 
         def h_steps(g, q):
             key = ("h", g, q)
@@ -251,7 +253,7 @@ def tile_spectral_transmittance_channel_flux_h3_kernel(
                     )
 
             def weigh():
-                live[key] = work.tile([P, QUARTER, 4], BF16, name="weighed", align_bytes=64)
+                live[key] = work.tile([P, QUARTER, 4], BF16, name="weighed", bufs=GROUPS, align_bytes=64)
                 nc.vector.tensor_tensor(
                     out=live[key][:], in0=live[key, "decay"][:],
                     in1=weights_psum[:, span(g, 4)].unsqueeze(1).to_broadcast([P, QUARTER, 4]), op=ALU.mult,
@@ -385,9 +387,15 @@ def tile_spectral_transmittance_channel_flux_h3_kernel(
             if first + count == 2:
                 steps["store", "codes", patch] = ([("pack", "y", part)], store_codes)
 
-        pairs = [(g, q) for q in range(QUARTERS) for g in range(0, GROUPS, 2)]
         last = GROUPS - 1
-        shared_pieces = [(last, 0)] + [(g, 1) for g in range(last)] + [(g, 2) for g in range(GROUPS)]
+        beside_two = [(last, 0), (0, 1)]
+        beside_four = {1: ((1, 1), (2, 1)), 2: ((0, 2), (1, 2)), 3: ((2, 2), (3, 2))}
+        shares = {piece: SHARE_OF_TWO for piece in beside_two}
+        paced_pieces = [(last - 1, 0)] + beside_two
+        for whole, partial in beside_four.values():
+            shares[whole] = PASS
+            shares[partial] = SHARE_AFTER_WHOLE
+            paced_pieces.append(whole)
         weights_steps()
         factor_steps()
         for q in range(QUARTERS):
@@ -395,7 +403,7 @@ def tile_spectral_transmittance_channel_flux_h3_kernel(
         for g in range(GROUPS):
             input_steps("absorption", g, 4, absorption_mx[g](span(0, PASS)))
             for c in range(THIRDS):
-                contrast_steps(g, c, (g, c) in shared_pieces, (g, c) == (last - 1, 0))
+                contrast_steps(g, c, shares.get((g, c), 0), (g, c) in paced_pieces)
             for q in range(QUARTERS):
                 h_steps(g, q)
 
@@ -403,20 +411,27 @@ def tile_spectral_transmittance_channel_flux_h3_kernel(
         for g in range(last):
             vector.extend([("weave", g, 0), ("pack", "absorption", g), ("pack", "contrast", g, 0)])
         gpsimd = []
-        for i, ((g, q), piece) in enumerate(zip(pairs, shared_pieces)):
-            gpsimd.append(("weave_first",) + piece)
-            steps[gpsimd[-1]][0].append(vector[-1])
-            vector.extend([("weigh", g, q), ("weigh", g + 1, q), ("weave",) + piece])
-            if i == 0:
-                vector.append(("pack", "absorption", last))
-            vector.extend([("pack", "h", g, q), ("pack", "h", g + 1, q)])
-            if i == 0:
-                vector.extend([("widen", "factors"), ("pack", "profiles", 1)])
-            if i == 1:
-                vector.extend([("shift", "factors"), ("pack", "profiles", 2)])
-            if i == 3:
-                vector.extend([("weave", last, 1), ("pack", "profiles", 3), ("pack", "contrast", last, 1)])
-            vector.append(("pack", "contrast") + piece)
+
+        def beside_gpsimd(pieces, groups, q):
+            gpsimd.extend(("weave_share",) + piece for piece in pieces)
+            steps[("weave_share",) + pieces[0]][0].append(vector[-1])
+            vector.extend(("weigh", g, q) for g in groups)
+
+        beside_gpsimd(beside_two[:1], [0, 1], 0)
+        vector.extend([("weave", last, 0), ("pack", "absorption", last), ("pack", "h", 0, 0), ("pack", "h", 1, 0)])
+        vector.extend([("widen", "factors"), ("pack", "profiles", 1), ("pack", "contrast", last, 0)])
+        beside_gpsimd(beside_two[1:], [2, 3], 0)
+        vector.extend([("weave", 0, 1), ("pack", "h", 2, 0), ("pack", "h", 3, 0)])
+        vector.extend([("shift", "factors"), ("pack", "contrast", 0, 1), ("pack", "profiles", 2)])
+        for q, (whole, partial) in beside_four.items():
+            beside_gpsimd([whole, partial], range(GROUPS), q)
+            vector.extend(("pack", "h", g, q) for g in range(GROUPS))
+            vector.append(("weave",) + partial)
+            if q == 1:
+                vector.extend([("weave", last, 1), ("pack", "profiles", 3), ("pack", "contrast") + partial])
+                vector.extend([("pack", "contrast") + whole, ("pack", "contrast", last, 1)])
+            else:
+                vector.extend([("pack", "contrast") + whole, ("pack", "contrast") + partial])
 
         patches = sorted(
             ((c, q) for c in range(THIRDS) for q in range(QUARTERS)),

from contextlib import ExitStack

import concourse.mybir as mybir
from concourse.masks import make_identity

LAYERS, POINTS, PROFILES, CHANNELS = 512, 2048, 1024, 1536
FLOPS = 2 * POINTS * LAYERS * PROFILES + 2 * PROFILES * POINTS * CHANNELS

F32 = mybir.dt.float32
BF16 = mybir.dt.bfloat16
U32 = mybir.dt.uint32
I32 = mybir.dt.int32
U8 = mybir.dt.uint8
FP8X4 = mybir.dt.float8_e4m3fn_x4
ACT = mybir.ActivationFunctionType
ALU = mybir.AluOpType

P = 128
PASS = 512
QUARTER = 256
GROUPS = POINTS // PASS
QUARTERS = PROFILES // QUARTER
THIRDS = CHANNELS // PASS
PATCHES = THIRDS * QUARTERS
CHANNEL_TILES = CHANNELS // P
PROFILE_TILES = PROFILES // P

SHARE_OF_TWO = 344
SHARE_AFTER_WHOLE = 272
TURNED_PATCHES = 5
FIRST_PLANES_ROUND = 6
ROTATING_BANKS = 7
LOAD_SLOTS = GROUPS + GROUPS * THIRDS
TURNED_TILES = 2 * PASS // P
DECAY_SLOTS = 6


def tile_spectral_transmittance_channel_flux_h3_kernel(
    tc, profiles, absorption, band_weights, contrast, offset, gain, angle_factor, out_0, out_1, out_2
):
    nc = tc.nc
    with ExitStack() as ctx:
        keep = ctx.enter_context(tc.tile_pool(name="keep", bufs=1))
        work = ctx.enter_context(tc.tile_pool(name="work", bufs=3))
        psum = ctx.enter_context(tc.psum_pool(name="psum", bufs=ROTATING_BANKS))
        ctx.enter_context(tc.manual_schedule())

        def span(index, width):
            return slice(index * width, (index + 1) * width)

        def bank(shape, name):
            return psum.tile(shape, F32, name=name, tag="bank")

        def quantize(codes, scales, grouped):
            nc.vector.quantize_mx(out=codes.bitcast(FP8X4), scales=scales, in_=grouped)

        def matmul(out, lhs, rhs, start, stop):
            nc.tensor.matmul_mx(
                out=out, lhsT=lhs[0].bitcast(FP8X4), lhsT_scale=lhs[1], rhs=rhs[0].bitcast(FP8X4), rhs_scale=rhs[1],
                start=start, stop=stop,
            )

        def packed(name, width):
            codes = keep.tile([P, width], U32, name=name + "_codes", align_bytes=64)
            scales = keep.tile([P, width], U8, name=name + "_scales", align_bytes=64)
            return lambda columns: (codes[:, columns], scales[:, columns])

        ident = keep.tile([P, P], F32, name="ident")
        make_identity(nc, ident[:])
        factor_rows = keep.tile([P, P], F32, name="factor_rows")
        nc.gpsimd.memset(factor_rows[:], 0.0)
        weights_wide = keep.tile([P, P], F32, name="weights_wide")
        nc.gpsimd.memset(weights_wide[:], 0.0)
        weights_turned = keep.tile([P, P], F32, name="weights_turned")
        weights_raw = keep.tile([P, GROUPS, 4], BF16, name="weights_raw")
        weights_psum = psum.tile([P, P], F32, name="weights_psum", bufs=1)
        gain_at, offset_at, angle_at = 0, TURNED_TILES, 2 * TURNED_TILES
        factor_count = angle_at + PROFILE_TILES
        factor_raw = keep.tile([factor_count, P], BF16, name="factor_raw")
        factors = keep.tile([P, factor_count], F32, name="factors")
        shift = keep.tile([P, TURNED_TILES], F32, name="shift")
        raw = {}

        def load_profiles(q):
            raw["profiles", q] = keep.tile([P, 2, LAYERS], BF16, name="raw_profiles%d" % q)
            rows = profiles[span(q, QUARTER), :]
            nc.sync.dma_start(out=raw["profiles", q][:], in_=rows.rearrange("(t m) k -> m t k", t=2))

        def load_absorption(g):
            raw["absorption", g] = keep.tile([P, 4, LAYERS], BF16, name="raw_absorption", tag="load", bufs=LOAD_SLOTS)
            rows = absorption[span(g, PASS), :]
            nc.sync.dma_start(out=raw["absorption", g][:], in_=rows.rearrange("(m t) k -> m t k", t=4))

        def load_contrast(g, c):
            raw["contrast", g, c] = keep.tile([P, 4, PASS], BF16, name="raw_contrast", tag="load", bufs=LOAD_SLOTS)
            piece = contrast[span(g, PASS), span(c, PASS)]
            nc.sync.dma_start(out=raw["contrast", g, c][:], in_=piece.rearrange("(p t) n -> p t n", t=4))

        load_profiles(0)
        for g in range(GROUPS):
            load_absorption(g)
            if g == 0:
                nc.sync.dma_start(out=weights_raw[:], in_=band_weights.rearrange("(g p t) -> p g t", g=GROUPS, t=4))
            load_contrast(g, 0)
        for vector_in, at, count in ((gain, gain_at, TURNED_TILES), (offset, offset_at, TURNED_TILES), (angle_factor, angle_at, PROFILE_TILES)):
            nc.sync.dma_start(out=factor_raw[at : at + count, :], in_=vector_in[: count * P].rearrange("(r i) -> r i", i=P))
        load_profiles(1)
        load_contrast(0, 1)
        load_profiles(2)
        for g in range(1, GROUPS):
            load_contrast(g, 1)
        load_profiles(3)
        for g in range(GROUPS):
            load_contrast(g, 2)
        gain_spread = keep.tile([P, CHANNELS], BF16, name="gain_spread")
        nc.sync.dma_start(out=gain_spread[:], in_=gain.partition_broadcast(P))
        offset_spread = keep.tile([P, CHANNELS], BF16, name="offset_spread")
        nc.sync.dma_start(out=offset_spread[:], in_=offset.partition_broadcast(P))

        profiles_mx = packed("profiles", PROFILES)
        absorption_mx = [packed("absorption%d" % g, PASS) for g in range(GROUPS)]
        h_mx = [packed("h%d" % g, PROFILES) for g in range(GROUPS)]
        contrast_mx = [packed("contrast%d" % g, CHANNELS) for g in range(GROUPS)]
        y_scales = keep.tile([P, PROFILES], U8, name="y_scales", align_bytes=64)

        steps = {}
        live = {}

        def chain(names, calls, needs):
            for name, call in zip(names, calls):
                steps[name] = (list(needs), call)
                needs = [name]

        def words_to_partitions(source, tiles, name):
            turned = bank([P, len(tiles), 2, P], name)
            for t, tile in enumerate(tiles):
                for u in range(2):
                    nc.tensor.transpose(turned[:, t, u, :], source(tile, u), ident[:])
            return turned

        def words_out(grouped, turned):
            nc.scalar.copy(
                out=grouped.bitcast(F32).rearrange("p (t m u) -> p t m u", m=P, u=2),
                in_=turned[:].rearrange("p t u m -> p t m u"),
            )

        def input_steps(kind, index, tiles, target):
            key = (kind, index)

            def turn():
                for pair in range(tiles // 2):
                    live[key, pair] = words_to_partitions(
                        lambda t, u: raw[key][:, t, :].bitcast(F32)[:, u : LAYERS // 2 : 2],
                        [2 * pair, 2 * pair + 1], "turned_input",
                    )

            def leave():
                live[key] = work.tile([P, tiles * PASS], BF16, name="grouped", align_bytes=64)
                for pair in range(tiles // 2):
                    words_out(live[key][:, span(pair, 2 * PASS)], live[key, pair])

            def pack():
                quantize(*target, live[key][:])

            chain([("turn",) + key, ("leave",) + key, ("pack",) + key], [turn, leave, pack], [])

        def weights_steps():
            def widen():
                nc.vector.tensor_copy(out=weights_wide[:, : 4 * GROUPS], in_=weights_raw[:].rearrange("p g t -> p (g t)"))

            def turn():
                live["weights"] = bank([P, P], "turned_weights")
                nc.tensor.transpose(live["weights"][:], weights_wide[:], ident[:])

            def leave():
                nc.scalar.copy(out=weights_turned[:], in_=live["weights"][:])

            def turn_back():
                nc.tensor.transpose(weights_psum[:], weights_turned[:], ident[:])

            names = [(verb, "weights") for verb in ("widen", "turn", "leave", "hold")]
            chain(names, [widen, turn, leave, turn_back], [])

        def factor_steps():
            def widen():
                nc.vector.tensor_copy(out=factor_rows[:factor_count, :], in_=factor_raw[:])

            def turn():
                live["factors"] = bank([P, P], "turned_factors")
                nc.tensor.transpose(live["factors"][:], factor_rows[:], ident[:])

            def leave():
                nc.scalar.copy(out=factors[:], in_=live["factors"][:, :factor_count])

            def product():
                nc.vector.tensor_tensor(
                    out=shift[:], in0=factors[:, gain_at:offset_at], in1=factors[:, offset_at:angle_at], op=ALU.mult
                )

            names = [(verb, "factors") for verb in ("widen", "turn", "leave", "shift")]
            chain(names, [widen, turn, leave, product], [])

        def contrast_steps(g, c, share, paced):
            key = ("contrast", g, c)

            def allocate():
                if paced:
                    live[key] = work.tile([P, 4 * PASS], BF16, name="grouped_paced", bufs=1, align_bytes=64)
                else:
                    live[key] = work.tile([P, 4 * PASS], BF16, name="grouped", align_bytes=64)

            def weave_share():
                allocate()
                nc.gpsimd.tensor_scalar(
                    out=live[key][:, : 4 * share].rearrange("p (n t) -> p n t", t=4),
                    in0=raw[key][:, :, :share].rearrange("p t n -> p n t"),
                    scalar1=1.0, scalar2=0.0, op0=ALU.mult, op1=ALU.add,
                )

            def weave():
                if share == 0:
                    allocate()
                nc.vector.tensor_copy(
                    out=live[key][:, 4 * share :].rearrange("p (n i t) -> p n t i", i=4, t=4),
                    in_=raw[key][:, :, share:].rearrange("p t (n i) -> p n t i", i=4),
                )

            def pack():
                quantize(*contrast_mx[g](span(c, PASS)), live[key][:])

            stages = [(("weave_share", g, c), weave_share)] if share > 0 else []
            if share < PASS:
                stages.append((("weave", g, c), weave))
            stages.append((("pack", "contrast", g, c), pack))
            chain([name for name, call in stages], [call for name, call in stages], [])

        def h_steps(g, q):
            key = ("h", g, q)

            def depth():
                for half in range(2):
                    live[key, half] = bank([P, 4, P], "tau")
                    for t in range(4):
                        matmul(live[key, half][:, t, :], absorption_mx[g](span(t, P)),
                               profiles_mx(span(2 * q + half, P)), True, True)

            def decay():
                live[key, "decay"] = work.tile([P, QUARTER, 4], F32, name="decay", bufs=DECAY_SLOTS)
                for half in range(2):
                    nc.scalar.activation(
                        out=live[key, "decay"][:, span(half, P), :], in_=live[key, half][:].rearrange("p t n -> p n t"),
                        func=ACT.Exp, scale=-1.0,
                    )

            def weigh():
                live[key] = work.tile([P, QUARTER, 4], BF16, name="weighed", bufs=GROUPS, align_bytes=64)
                nc.vector.tensor_tensor(
                    out=live[key][:], in0=live[key, "decay"][:],
                    in1=weights_psum[:, span(g, 4)].unsqueeze(1).to_broadcast([P, QUARTER, 4]), op=ALU.mult,
                )

            def pack():
                quantize(*h_mx[g](span(q, QUARTER)), live[key][:].rearrange("p n t -> p (n t)"))

            chain([("depth", g, q), ("decay", g, q)], [depth, decay], [("pack", "absorption", g), ("pack", "profiles", q)])
            chain([("weigh", g, q), ("pack", "h", g, q)], [weigh, pack], [("decay", g, q), ("hold", "weights")])

        def operands(c, q):
            return [("pack", "h", g, q) for g in range(GROUPS)] + [("pack", "contrast", g, c) for g in range(GROUPS)]

        def new_y(patch):
            live["y", patch] = keep.tile([P, 2, PASS], F32, name="y", tag="load", bufs=LOAD_SLOTS)

        def angle(q, half):
            column = angle_at + 2 * q + half
            return factors[:, column : column + 1]

        def turned_patch_steps(patch, c, q):
            def product(half):
                live["flux", patch, half] = bank([P, 2, QUARTER], "flux_turned")
                for i in range(2):
                    for g in range(GROUPS):
                        matmul(live["flux", patch, half][:, i, :], contrast_mx[g](span(4 * c + 2 * half + i, P)),
                               h_mx[g](span(q, QUARTER)), g == 0, g == GROUPS - 1)

            def scale(half):
                if half == 0:
                    live["scaled", patch] = work.tile([P, 4, QUARTER], F32, name="scaled")
                for i in range(2):
                    tile = 4 * c + 2 * half + i
                    nc.scalar.activation(
                        out=live["scaled", patch][:, 2 * half + i, :], in_=live["flux", patch, half][:, i, :],
                        func=ACT.Identity, scale=factors[:, gain_at + tile : gain_at + tile + 1], bias=shift[:, tile : tile + 1],
                    )

            def turn():
                for half in range(2):
                    live["back", patch, half] = bank([P, 4, P], "turned_back")
                    for i in range(4):
                        nc.tensor.transpose(
                            live["back", patch, half][:, i, :], live["scaled", patch][:, i, span(half, P)], ident[:]
                        )

            def leave():
                new_y(patch)
                for half in range(2):
                    nc.scalar.activation(
                        out=live["y", patch][:, half, :], in_=live["back", patch, half][:].rearrange("p i n -> p (i n)"),
                        func=ACT.Copy, scale=angle(q, half),
                    )

            for half in range(2):
                chain([("product", patch, half), ("scale", patch, half)],
                      [lambda half=half: product(half), lambda half=half: scale(half)],
                      operands(c, q) + [("shift", "factors")])
            chain([("turn", "back", patch), ("leave", "back", patch)], [turn, leave],
                  [("scale", patch, 0), ("scale", patch, 1)])
            return [("leave", "back", patch)]

        def straight_patch_steps(patch, c, q):
            def product(half):
                live["flux", patch, half] = bank([P, PASS], "flux")
                for g in range(GROUPS):
                    matmul(live["flux", patch, half][:], h_mx[g](span(2 * q + half, P)),
                           contrast_mx[g](span(c, PASS)), g == 0, g == GROUPS - 1)

            def add(half):
                live["sum", patch, half] = work.tile([P, PASS], F32, name="summed")
                nc.vector.tensor_tensor(
                    out=live["sum", patch, half][:], in0=live["flux", patch, half][:],
                    in1=offset_spread[:, span(c, PASS)], op=ALU.add,
                )

            def finish(half):
                if half == 0:
                    new_y(patch)
                nc.vector.scalar_tensor_tensor(
                    out=live["y", patch][:, half, :], in0=live["sum", patch, half][:], scalar=angle(q, half),
                    in1=gain_spread[:, span(c, PASS)], op0=ALU.mult, op1=ALU.mult,
                )

            for half in range(2):
                chain([("product", patch, half), ("add", patch, half), ("finish", patch, half)],
                      [lambda half=half: product(half), lambda half=half: add(half), lambda half=half: finish(half)],
                      operands(c, q))
            return [("finish", patch, 0), ("finish", patch, 1)]

        def output_steps(part, c, q, first, count, done):
            patch = min(part, PATCHES - 1)
            tiles = slice(first, first + count)
            rows = slice(q * QUARTER + first * P, q * QUARTER + (first + count) * P)

            def store_y():
                nc.sync.dma_start(
                    out=out_0[rows, span(c, PASS)].rearrange("(t p) n -> p t n", t=count), in_=live["y", patch][:, tiles, :]
                )

            def round_y():
                live["rounded", part] = work.tile([P, count * PASS], BF16, name="rounded", bufs=4)
                copy = nc.vector.tensor_copy if patch == PATCHES - 1 else nc.scalar.copy
                copy(
                    out=live["rounded", part][:].rearrange("p (t u m e) -> p t u m e", t=count, u=2, e=2),
                    in_=live["y", patch][:, tiles, :].rearrange("p t (m u e) -> p t u m e", u=2, e=2),
                )

            def turn():
                words = live["rounded", part][:].bitcast(F32)
                live["planes", part] = words_to_partitions(lambda t, u: words[:, span(2 * t + u, P)], range(count), "turned_y")

            def leave():
                live["grouped", part] = work.tile([P, count * PASS], BF16, name="grouped_y", bufs=4, align_bytes=64)
                words_out(live["grouped", part][:], live["planes", part])

            def pack():
                if first == 0:
                    live["codes", patch] = work.tile([P, QUARTER], U32, name="y_codes", bufs=4, align_bytes=64)
                codes = live["codes", patch][:, first * P : (first + count) * P]
                quantize(codes, y_scales[4 * c : P, rows], live["grouped", part][:])

            def store_codes():
                words = out_1[c].rearrange("p m t -> p (m t)").bitcast(I32)
                nc.sync.dma_start(out=words[:, span(q, QUARTER)], in_=live["codes", patch][:].bitcast(I32))

            steps["store", "y", part] = (done, store_y)
            chain([("round", part), ("turn", "y", part), ("leave", "y", part), ("pack", "y", part)],
                  [round_y, turn, leave, pack], done)
            if first + count == 2:
                steps["store", "codes", patch] = ([("pack", "y", part)], store_codes)

        last = GROUPS - 1
        beside_two = [(last, 0), (0, 1)]
        beside_four = {1: ((1, 1), (2, 1)), 2: ((0, 2), (1, 2)), 3: ((2, 2), (3, 2))}
        shares = {piece: SHARE_OF_TWO for piece in beside_two}
        paced_pieces = [(last - 1, 0)] + beside_two
        for whole, partial in beside_four.values():
            shares[whole] = PASS
            shares[partial] = SHARE_AFTER_WHOLE
            paced_pieces.append(whole)
        weights_steps()
        factor_steps()
        for q in range(QUARTERS):
            input_steps("profiles", q, 2, profiles_mx(span(q, QUARTER)))
        for g in range(GROUPS):
            input_steps("absorption", g, 4, absorption_mx[g](span(0, PASS)))
            for c in range(THIRDS):
                contrast_steps(g, c, shares.get((g, c), 0), (g, c) in paced_pieces)
            for q in range(QUARTERS):
                h_steps(g, q)

        vector = [("widen", "weights"), ("pack", "profiles", 0)]
        for g in range(last):
            vector.extend([("weave", g, 0), ("pack", "absorption", g), ("pack", "contrast", g, 0)])
        gpsimd = []

        def beside_gpsimd(pieces, groups, q):
            gpsimd.extend(("weave_share",) + piece for piece in pieces)
            steps[("weave_share",) + pieces[0]][0].append(vector[-1])
            vector.extend(("weigh", g, q) for g in groups)

        beside_gpsimd(beside_two[:1], [0, 1], 0)
        vector.extend([("weave", last, 0), ("pack", "absorption", last), ("pack", "h", 0, 0), ("pack", "h", 1, 0)])
        vector.extend([("widen", "factors"), ("pack", "profiles", 1), ("pack", "contrast", last, 0)])
        beside_gpsimd(beside_two[1:], [2, 3], 0)
        vector.extend([("weave", 0, 1), ("pack", "h", 2, 0), ("pack", "h", 3, 0)])
        vector.extend([("shift", "factors"), ("pack", "contrast", 0, 1), ("pack", "profiles", 2)])
        for q, (whole, partial) in beside_four.items():
            beside_gpsimd([whole, partial], range(GROUPS), q)
            vector.extend(("pack", "h", g, q) for g in range(GROUPS))
            vector.append(("weave",) + partial)
            if q == 1:
                vector.extend([("weave", last, 1), ("pack", "profiles", 3), ("pack", "contrast") + partial])
                vector.extend([("pack", "contrast") + whole, ("pack", "contrast", last, 1)])
            else:
                vector.extend([("pack", "contrast") + whole, ("pack", "contrast") + partial])

        patches = sorted(
            ((c, q) for c in range(THIRDS) for q in range(QUARTERS)),
            key=lambda cq: max(vector.index(name) for name in operands(*cq)),
        )
        for patch, (c, q) in enumerate(patches):
            kind = turned_patch_steps if patch < TURNED_PATCHES else straight_patch_steps
            done = kind(patch, c, q)
            if patch < PATCHES - 1:
                output_steps(patch, c, q, 0, 2, done)
            else:
                output_steps(patch, c, q, 0, 1, done[:1])
                output_steps(patch + 1, c, q, 1, 1, done[1:])
        parts = PATCHES + 1

        tensor = [("turn", "profiles", 0), ("turn", "absorption", 0), ("turn", "weights")]
        for g in range(GROUPS):
            if g < last:
                tensor.append(("turn", "absorption", g + 1))
            if g == 0:
                tensor.append(("hold", "weights"))
            if g >= 2:
                tensor.append(("turn", "profiles", g - 1))
            tensor.append(("depth", g, 0))
        tensor.append(("turn", "factors"))
        depth_round = {(g, q): q - 1 if q < 3 else 2 + g // 2 for g in range(GROUPS) for q in range(1, QUARTERS)}
        planes_round = [max(FIRST_PLANES_ROUND + part // 2, min(part, PATCHES - 1) + 2) for part in range(parts)]
        rounds = planes_round[-1] + 1
        round_ends = []
        for r in range(rounds):
            depths = [("depth", g, q) for (g, q) in sorted(depth_round) if depth_round[g, q] == r]
            products = [("product", r, half) for half in range(2)] if r < PATCHES else []
            turns = [("turn", "back", r - 1)] if 1 <= r <= TURNED_PATCHES else []
            turns.extend(("turn", "y", part) for part in range(parts) if planes_round[part] == r)
            if r == 0:
                turns.append(("turn", "profiles", 3))
            tensor.extend(depths + turns + products if r == 1 else depths + products + turns)
            round_ends.append(tensor[-1])

        def emptied_by(name):
            if name[0] == "turn":
                return ("leave",) + name[1:]
            if name[0] == "depth":
                return ("decay",) + name[1:]
            return ("scale" if name[1] < TURNED_PATCHES else "add",) + name[1:]

        fills = [name for name in tensor if name[0] != "hold"]
        scalar = []
        for name in fills:
            if emptied_by(name)[0] != "add":
                scalar.append(emptied_by(name))
            if name in round_ends:
                ahead = round_ends.index(name) + 2
                scalar.extend(("round", patch) for patch in range(PATCHES - 1) if planes_round[patch] == ahead)

        stores = []
        for r in range(rounds + 1):
            packs = [("pack", "y", part) for part in range(parts) if planes_round[part] == r - 1]
            if TURNED_PATCHES <= r < PATCHES:
                vector.extend([("add", r, 0)] + packs[:1] + [("add", r, 1), ("finish", r, 0)] + packs[1:] + [("finish", r, 1)])
            else:
                vector.extend(packs)
            if r == PATCHES - 1:
                vector.extend([("round", r), ("round", r + 1)])
            stores.extend(("store", "codes", patch) for patch in range(PATCHES) if planes_round[patch] == r - 2)
            if 1 <= r <= parts:
                stores.append(("store", "y", r - 1))
        stores.append(("store", "codes", PATCHES - 1))

        filled = []
        for name in fills:
            banks = 2 if name[0] == "depth" or name[:2] in (("turn", "absorption"), ("turn", "back")) else 1
            first = len(filled) - ROTATING_BANKS
            steps[name][0].extend(filled[i] for i in range(max(first, 0), max(first + banks, 0)))
            filled.extend([emptied_by(name)] * banks)
        decays = [name for name in scalar if name[0] == "decay"]
        for earlier, later in zip(decays, decays[DECAY_SLOTS:]):
            steps[later][0].append(("weigh",) + earlier[1:])

        programs = [gpsimd, vector, scalar, tensor, stores]
        heads = [0] * len(programs)
        written = set()
        while any(head < len(program) for head, program in zip(heads, programs)):
            for i, program in enumerate(programs):
                while heads[i] < len(program) and all(name in written for name in steps[program[heads[i]]][0]):
                    steps[program[heads[i]]][1]()
                    written.add(program[heads[i]])
                    heads[i] = heads[i] + 1

        scale_rows = out_2.bitcast(I32)
        for quadrant in range(4):
            nc.scalar.dma_start(
                out=scale_rows[:, span(quadrant, 4), :],
                in_=y_scales[32 * quadrant : 32 * quadrant + 4 * THIRDS, :].bitcast(I32),
            )
